import numpy as np
import ml_dtypes


def mxq(x, axis, fmt="e4m3"):
    dtype, down = {"e4m3": (ml_dtypes.float8_e4m3fn, 7), "e5m2": (ml_dtypes.float8_e5m2, 14)}[fmt]
    v = np.moveaxis(np.asarray(x, np.float32).astype(ml_dtypes.bfloat16).astype(np.float64), axis, -1)
    blocks = v.reshape(v.shape[:-1] + (-1, 32))
    amax = np.abs(blocks).max(-1, keepdims=True)
    byte = np.maximum(np.where(amax > 0, np.frexp(amax)[1] - 1 + 127, 0) - down, 1)
    scale = np.exp2(byte - 127.0)
    codes = (blocks / scale).astype(np.float32).astype(dtype).astype(np.float64)
    return np.moveaxis((codes * scale).reshape(v.shape), -1, axis)


WIDE = False


def mx_kscale(k):
    if not WIDE:
        return np.ones(k)
    levels = np.array([10, -10, 5, -5, 0])
    if k % 512:
        return np.exp2(np.random.permutation(np.resize(levels, k // 32))).repeat(32)
    a = np.empty((k // 512, 16))
    for p in range(k // 512):
        a[p, :8] = np.random.permutation(np.resize(levels, 8))
        for g in range(8):
            far = levels[np.abs(levels - a[p, g]) >= 10]
            a[p, g + 8] = far[np.random.randint(len(far))]
    return np.exp2(a.ravel()).repeat(32)


def f64(x):
    return np.asarray(x).astype(np.float64)


def striped8(idx):
    return np.concatenate([v.reshape(-1, 16).T for v in idx]).astype(np.uint16)


def unstriped8(offs):
    return np.stack([offs[16 * g:16 * g + 16].T.reshape(-1) for g in range(8)]).astype(np.int64)


E2M1 = np.array([0.0, 0.5, 1.0, 1.5, 2.0, 3.0, 4.0, 6.0, -0.0, -0.5, -1.0, -1.5, -2.0, -3.0, -4.0, -6.0])


def pack_weight(w, fmt):
    k, n = w.shape
    w = f64(np.asarray(w, np.float32).astype(ml_dtypes.bfloat16)).reshape(k // 32, 32, n)
    amax = np.abs(w).max(1)
    if fmt == "e4m3":
        byte = np.frexp(amax)[1] - 1 + 127 - 7
    else:
        mant, ex = np.frexp(amax / 6.0)
        byte = np.where(mant > 0.5, ex, ex - 1) + 127
    byte = np.clip(np.where(amax > 0, byte, 1), 1, 254)
    scaled = (w * np.exp2(127.0 - byte)[:, None, :]).reshape(k, n).astype(np.float32)
    by_word = np.ascontiguousarray(scaled.reshape(k // 512, 128, 4, n).transpose(0, 1, 3, 2))
    if fmt == "e4m3":
        words = by_word.astype(ml_dtypes.float8_e4m3fn).view(np.uint8)
    else:
        c = by_word.astype(ml_dtypes.float4_e2m1fn).view(np.uint8) & 0xF
        words = (c[..., 0::2] | (c[..., 1::2] << 4)).reshape(k // 512, 128, 2 * n)
    return np.ascontiguousarray(words), np.ascontiguousarray(byte.astype(np.uint8).reshape(k // 512, 16, n))


def unpack_weight(words, scales, fmt):
    g, _, n = scales.shape
    words = np.ascontiguousarray(words).reshape(g, 128, n, -1)
    if fmt == "e4m3":
        vals = words.view(ml_dtypes.float8_e4m3fn).astype(np.float64)
    else:
        nib = np.empty((g, 128, n, 4), np.uint8)
        nib[..., 0::2] = words & 0xF
        nib[..., 1::2] = words >> 4
        vals = E2M1[nib]
    vals = vals * np.repeat(np.exp2(scales.astype(np.float64) - 127.0), 8, axis=1)[..., None]
    return vals.transpose(0, 1, 3, 2).reshape(g * 512, n)


def gelu(v):
    return 0.5 * v * (1.0 + np.tanh(np.sqrt(2.0 / np.pi) * (v + 0.044715 * v**3)))


K, M, T, S = 1024, 512, 512, 256


def setup_inputs():
    n = np.random.standard_normal
    s = mx_kscale(K)[:, None]
    u = mx_kscale(512)[:, None]
    p_w2 = pack_weight(1.4 * n((512, M)) / np.sqrt(512) / u, "e2m1")
    return {
        "x": (n((K, S)) * s).astype(np.float32),
        "w1": (n((K, 512)) / np.sqrt(K) / s * u.T).astype(np.float32),
        "w2_words": p_w2[0],
        "w2_scales": p_w2[1],
        "b": (0.3 * n(512)).astype(np.float32),
        "wgo": np.repeat(np.random.uniform(0.5, 2.0, (8, S)), 16, axis=0).astype(np.float32),
        "offs": striped8(np.stack([np.random.permutation(T)[:S] for _ in range(8)])),
    }


def reference(x, w1, w2_words, w2_scales, b, wgo, offs):
    x_ = mxq(f64(x), 0, "e4m3")
    w1_ = mxq(f64(w1), 0, "e4m3")
    w2_ = unpack_weight(w2_words, w2_scales, "e2m1")
    h_ = mxq(np.maximum(w1_.T @ x_, 0.0), 0, "e4m3")
    y = w2_.T @ h_
    place = unstriped8(offs)[np.arange(M) % 128 // 16]
    out = np.zeros((M, T))
    out[np.arange(M)[:, None], place] = f64(wgo)[np.arange(M) % 128] * (gelu(y + f64(b)[:, None]))
    return out

@@ -1,0 +1,182 @@
+from contextlib import ExitStack
+
+import concourse.mybir as mybir
+from concourse.masks import make_identity
+
+K, R, M, T, S = 1024, 512, 512, 512, 256
+FLOPS = 2 * K * R * S + 2 * R * M * S
+
+F32 = mybir.dt.float32
+BF16 = mybir.dt.bfloat16
+I32 = mybir.dt.int32
+U32 = mybir.dt.uint32
+U16 = mybir.dt.uint16
+U8 = mybir.dt.uint8
+FP8X4 = mybir.dt.float8_e4m3fn_x4
+FP4X4 = mybir.dt.float4_e2m1fn_x4
+ACT = mybir.ActivationFunctionType
+MULT = mybir.AluOpType.mult
+
+P = 128
+PACK = 4
+K_PASS = P * PACK
+PASSES = K // K_PASS
+HALF = 128
+HALVES = S // HALF
+OUT_TILES = M // P
+
+W1_CHUNKS = [(0, 0, 512, 2), (1, 0, 256, 3), (1, 256, 256, 3)]
+
+
+def tile_list_hscat_m_gelu_kernel(tc, x, w1, w2_words, w2_scales, b, wgo, offs, out):
+    nc = tc.nc
+    with ExitStack() as ctx:
+        keep = ctx.enter_context(tc.tile_pool(name="keep", bufs=1))
+        psum = ctx.enter_context(tc.psum_pool(name="psum", bufs=1))
+        psum_y = ctx.enter_context(tc.psum_pool(name="psum_y", bufs=5))
+
+        offsets = keep.tile([P, S // 16], U16, name="offsets")
+
+        w1_raw = []
+        for i, (a, c0, cols, on_v) in enumerate(W1_CHUNKS):
+            raw = keep.tile([P, PACK, cols], F32, name="w1_raw%d" % i)
+            nc.sync.dma_start(
+                out=raw[:],
+                in_=w1[a * K_PASS : (a + 1) * K_PASS, c0 : c0 + cols].rearrange("(p j) c -> p j c", j=PACK),
+            )
+            w1_raw.append(raw)
+
+        x_raw = {}
+
+        def load_x(h, a):
+            raw = keep.tile([P, PACK, HALF], F32, name="x_raw%d%d" % (h, a))
+            nc.sync.dma_start(
+                out=raw[:],
+                in_=x[a * K_PASS : (a + 1) * K_PASS, h * HALF : (h + 1) * HALF].rearrange("(p j) c -> p j c", j=PACK),
+            )
+            x_raw[(h, a)] = raw
+
+        load_x(0, 0)
+        load_x(0, 1)
+        nc.sync.dma_start(offsets[:], offs)
+        w2_codes = keep.tile([P, 2 * M], U8, name="w2_codes", align_bytes=64)
+        nc.sync.dma_start(out=w2_codes[:].bitcast(I32), in_=w2_words[0].bitcast(I32))
+        load_x(1, 0)
+        load_x(1, 1)
+        weights = keep.tile([P, S], F32, name="weights")
+        nc.sync.dma_start(out=weights[:], in_=wgo)
+
+        warm_in = keep.tile([P, 1], F32, name="warm_in")
+        warm_out = keep.tile([P, 1], F32, name="warm_out")
+        nc.vector.memset(warm_in[:], 0.0)
+        nc.scalar.activation(out=warm_out[:], in_=warm_in[:], func=ACT.Gelu_apprx_tanh)
+
+        w2_plane = keep.tile([P, M], U8, name="w2_plane", align_bytes=64)
+        nc.vector.memset(w2_plane[:].bitcast(I32), 0)
+        b_rows = keep.tile([P, P], F32, name="b_rows")
+        nc.vector.memset(b_rows[:], 0.0)
+        nc.gpsimd.dma_start(out=b_rows[0:OUT_TILES, :], in_=b.rearrange("(c p) -> c p", p=P))
+        for q in range(4):
+            nc.gpsimd.dma_start(
+                out=w2_plane[32 * q : 32 * q + 4, :].bitcast(I32),
+                in_=w2_scales[0, 4 * q : 4 * q + 4, :].bitcast(I32),
+            )
+        ident = keep.tile([P, P], F32, name="ident")
+        make_identity(nc, ident[:])
+        b_turned = psum.tile([P, P], F32, name="b_turned")
+        nc.tensor.transpose(b_turned[:], b_rows[:], ident[:])
+        bias = keep.tile([P, OUT_TILES], F32, name="bias")
+        nc.scalar.copy(out=bias[:], in_=b_turned[:, 0:OUT_TILES])
+
+        windows = []
+        for c in range(OUT_TILES):
+            window = keep.tile([P, T], F32, name="window%d" % c)
+            nc.vector.memset(window[:], 0.0)
+            windows.append(window)
+
+        w1_codes = keep.tile([P, PASSES, PACK, P], U32, name="w1_codes", align_bytes=64)
+        w1_plane = keep.tile([P, PASSES, PACK, P], U8, name="w1_plane", align_bytes=64)
+        for i, (a, c0, cols, on_vector) in enumerate(W1_CHUNKS):
+            ms = cols // PACK
+            m0 = c0 // PACK
+            src = w1_raw[i][:].rearrange("p j (m t) -> p m j t", t=PACK)
+            part_v = keep.tile([P, on_vector, ms, PACK], BF16, name="w1_v%d" % i, align_bytes=64)
+            part_s = keep.tile([P, PACK - on_vector, ms, PACK], BF16, name="w1_s%d" % i, align_bytes=64)
+            nc.vector.tensor_copy(out=part_v[:].rearrange("p t m j -> p m j t"), in_=src[:, :, :, 0:on_vector])
+            nc.scalar.copy(out=part_s[:].rearrange("p t m j -> p m j t"), in_=src[:, :, :, on_vector:PACK])
+            for t in range(PACK):
+                grouped = part_v[:, t] if t < on_vector else part_s[:, t - on_vector]
+                nc.vector.quantize_mx(
+                    out=w1_codes[:, a, t, m0 : m0 + ms].bitcast(FP8X4),
+                    scales=w1_plane[:, a, t, m0 : m0 + ms],
+                    in_=grouped.rearrange("p m j -> p (m j)"),
+                )
+
+        acts = {}
+        for h in range(HALVES):
+            x_codes = keep.tile([P, PASSES, HALF], U32, name="x_codes%d" % h, align_bytes=64)
+            x_plane = keep.tile([P, PASSES, HALF], U8, name="x_plane%d" % h, align_bytes=64)
+            x_grouped = []
+            for a in range(PASSES):
+                grouped = keep.tile([P, HALF, PACK], BF16, name="x_grouped%d%d" % (h, a), align_bytes=64)
+                dst = grouped[:].rearrange("p (c i) j -> p c j i", i=4)
+                src = x_raw[(h, a)][:].rearrange("p j (c i) -> p c j i", i=4)
+                if (h, a) == (0, 0):
+                    nc.scalar.copy(out=dst, in_=src)
+                else:
+                    nc.vector.tensor_copy(out=dst, in_=src)
+                x_grouped.append(grouped)
+            for a in range(PASSES):
+                nc.vector.quantize_mx(
+                    out=x_codes[:, a, :].bitcast(FP8X4),
+                    scales=x_plane[:, a, :],
+                    in_=x_grouped[a][:].rearrange("p c j -> p (c j)"),
+                )
+
+            h_acc = psum.tile([P, PACK, HALF], F32, name="h_acc%d" % h)
+            for t in range(PACK):
+                for a in range(PASSES):
+                    nc.tensor.matmul_mx(
+                        out=h_acc[:, t, :],
+                        lhsT=w1_codes[:, a, t, :].bitcast(FP8X4),
+                        lhsT_scale=w1_plane[:, a, t, :],
+                        rhs=x_codes[:, a, :].bitcast(FP8X4),
+                        rhs_scale=x_plane[:, a, :],
+                        start=(a == 0),
+                        stop=(a == PASSES - 1),
+                    )
+            h_grouped = keep.tile([P, HALF, PACK], BF16, name="h_grouped%d" % h, align_bytes=64)
+            nc.scalar.activation(out=h_grouped[:], in_=h_acc[:].rearrange("p t c -> p c t"), func=ACT.Relu)
+            h_codes = keep.tile([P, HALF], U32, name="h_codes%d" % h, align_bytes=64)
+            h_plane = keep.tile([P, HALF], U8, name="h_plane%d" % h, align_bytes=64)
+            nc.vector.quantize_mx(
+                out=h_codes[:].bitcast(FP8X4),
+                scales=h_plane[:],
+                in_=h_grouped[:].rearrange("p c t -> p (c t)"),
+            )
+            for c in range(OUT_TILES):
+                y_acc = psum_y.tile([P, HALF], F32, name="y_acc")
+                nc.tensor.matmul_mx(
+                    out=y_acc[:],
+                    lhsT=w2_codes[:, 2 * P * c : 2 * P * (c + 1)].bitcast(FP4X4),
+                    lhsT_scale=w2_plane[:, P * c : P * (c + 1)],
+                    rhs=h_codes[:].bitcast(FP8X4),
+                    rhs_scale=h_plane[:],
+                    start=True,
+                    stop=True,
+                )
+                act = keep.tile([P, HALF], F32, name="act%d%d" % (h, c))
+                nc.scalar.activation(out=act[:], in_=y_acc[:], func=ACT.Gelu_apprx_tanh, bias=bias[:, c : c + 1])
+                acts[(h, c)] = act
+
+        for h in range(HALVES):
+            list_cols = slice(h * HALF // 16, (h + 1) * HALF // 16)
+            for c in range(OUT_TILES):
+                nc.vector.tensor_tensor(
+                    windows[c][:].indirect(offsets[:, list_cols]),
+                    acts[(h, c)][:],
+                    weights[:, h * HALF : (h + 1) * HALF],
+                    MULT,
+                )
+                if h == HALVES - 1:
+                    nc.sync.dma_start(out=out[P * c : P * (c + 1), :], in_=windows[c][:])

@@ -26,6 +26,7 @@ HALVES = S // HALF
 OUT_TILES = M // P
 
 W1_CHUNKS = [(0, 0, 512, 2), (1, 0, 256, 3), (1, 256, 256, 3)]
+X_ON_VECTOR = {(0, 0): 48, (0, 1): 72, (1, 0): 128, (1, 1): 0}
 
 
 def tile_list_hscat_m_gelu_kernel(tc, x, w1, w2_words, w2_scales, b, wgo, offs, out):
@@ -33,9 +34,17 @@ def tile_list_hscat_m_gelu_kernel(tc, x, w1, w2_words, w2_scales, b, wgo, offs, 
     with ExitStack() as ctx:
         keep = ctx.enter_context(tc.tile_pool(name="keep", bufs=1))
         psum = ctx.enter_context(tc.psum_pool(name="psum", bufs=1))
-        psum_y = ctx.enter_context(tc.psum_pool(name="psum_y", bufs=5))
 
         offsets = keep.tile([P, S // 16], U16, name="offsets")
+
+        w2_plane = keep.tile([P, M], U8, name="w2_plane", align_bytes=64)
+        nc.vector.memset(w2_plane[:].bitcast(I32), 0)
+        b_rows = keep.tile([P, P], F32, name="b_rows")
+        nc.vector.memset(b_rows[:], 0.0)
+        warm_in = keep.tile([P, 1], F32, name="warm_in")
+        warm_out = keep.tile([P, 1], F32, name="warm_out")
+        nc.vector.memset(warm_in[:], 0.0)
+        nc.scalar.activation(out=warm_out[:], in_=warm_in[:], func=ACT.Gelu_apprx_tanh)
 
         w1_raw = []
         for i, (a, c0, cols, on_v) in enumerate(W1_CHUNKS):
@@ -45,6 +54,13 @@ def tile_list_hscat_m_gelu_kernel(tc, x, w1, w2_words, w2_scales, b, wgo, offs, 
                 in_=w1[a * K_PASS : (a + 1) * K_PASS, c0 : c0 + cols].rearrange("(p j) c -> p j c", j=PACK),
             )
             w1_raw.append(raw)
+            if i == 0:
+                nc.sync.dma_start(out=b_rows[0:OUT_TILES, :], in_=b.rearrange("(c p) -> c p", p=P))
+                for q in range(4):
+                    nc.sync.dma_start(
+                        out=w2_plane[32 * q : 32 * q + 4, :].bitcast(I32),
+                        in_=w2_scales[0, 4 * q : 4 * q + 4, :].bitcast(I32),
+                    )
 
         x_raw = {}
 
@@ -66,21 +82,6 @@ def tile_list_hscat_m_gelu_kernel(tc, x, w1, w2_words, w2_scales, b, wgo, offs, 
         weights = keep.tile([P, S], F32, name="weights")
         nc.sync.dma_start(out=weights[:], in_=wgo)
 
-        warm_in = keep.tile([P, 1], F32, name="warm_in")
-        warm_out = keep.tile([P, 1], F32, name="warm_out")
-        nc.vector.memset(warm_in[:], 0.0)
-        nc.scalar.activation(out=warm_out[:], in_=warm_in[:], func=ACT.Gelu_apprx_tanh)
-
-        w2_plane = keep.tile([P, M], U8, name="w2_plane", align_bytes=64)
-        nc.vector.memset(w2_plane[:].bitcast(I32), 0)
-        b_rows = keep.tile([P, P], F32, name="b_rows")
-        nc.vector.memset(b_rows[:], 0.0)
-        nc.gpsimd.dma_start(out=b_rows[0:OUT_TILES, :], in_=b.rearrange("(c p) -> c p", p=P))
-        for q in range(4):
-            nc.gpsimd.dma_start(
-                out=w2_plane[32 * q : 32 * q + 4, :].bitcast(I32),
-                in_=w2_scales[0, 4 * q : 4 * q + 4, :].bitcast(I32),
-            )
         ident = keep.tile([P, P], F32, name="ident")
         make_identity(nc, ident[:])
         b_turned = psum.tile([P, P], F32, name="b_turned")
@@ -112,62 +113,95 @@ def tile_list_hscat_m_gelu_kernel(tc, x, w1, w2_words, w2_scales, b, wgo, offs, 
                     in_=grouped.rearrange("p m j -> p (m j)"),
                 )
 
-        acts = {}
-        for h in range(HALVES):
-            x_codes = keep.tile([P, PASSES, HALF], U32, name="x_codes%d" % h, align_bytes=64)
-            x_plane = keep.tile([P, PASSES, HALF], U8, name="x_plane%d" % h, align_bytes=64)
+        def quantise_x(h):
+            codes = keep.tile([P, PASSES, HALF], U32, name="x_codes%d" % h, tag="late" if h == 0 else "xb_codes", align_bytes=64)
+            plane = keep.tile([P, PASSES, HALF], U8, name="x_plane%d" % h, align_bytes=64)
             x_grouped = []
             for a in range(PASSES):
-                grouped = keep.tile([P, HALF, PACK], BF16, name="x_grouped%d%d" % (h, a), align_bytes=64)
+                name = "x_grouped%d%d" % (h, a)
+                grouped = keep.tile([P, HALF, PACK], BF16, name=name, tag="late" if (h, a) == (1, 1) else name, align_bytes=64)
                 dst = grouped[:].rearrange("p (c i) j -> p c j i", i=4)
                 src = x_raw[(h, a)][:].rearrange("p j (c i) -> p c j i", i=4)
-                if (h, a) == (0, 0):
-                    nc.scalar.copy(out=dst, in_=src)
-                else:
-                    nc.vector.tensor_copy(out=dst, in_=src)
+                cut = X_ON_VECTOR[(h, a)] // 4
+                if cut > 0:
+                    nc.vector.tensor_copy(out=dst[:, 0:cut], in_=src[:, 0:cut])
+                if cut < HALF // 4:
+                    nc.scalar.copy(out=dst[:, cut:], in_=src[:, cut:])
                 x_grouped.append(grouped)
             for a in range(PASSES):
                 nc.vector.quantize_mx(
-                    out=x_codes[:, a, :].bitcast(FP8X4),
-                    scales=x_plane[:, a, :],
+                    out=codes[:, a, :].bitcast(FP8X4),
+                    scales=plane[:, a, :],
                     in_=x_grouped[a][:].rearrange("p c j -> p (c j)"),
                 )
+            return codes, plane
 
-            h_acc = psum.tile([P, PACK, HALF], F32, name="h_acc%d" % h)
-            for t in range(PACK):
-                for a in range(PASSES):
-                    nc.tensor.matmul_mx(
-                        out=h_acc[:, t, :],
-                        lhsT=w1_codes[:, a, t, :].bitcast(FP8X4),
-                        lhsT_scale=w1_plane[:, a, t, :],
-                        rhs=x_codes[:, a, :].bitcast(FP8X4),
-                        rhs_scale=x_plane[:, a, :],
-                        start=(a == 0),
-                        stop=(a == PASSES - 1),
-                    )
-            h_grouped = keep.tile([P, HALF, PACK], BF16, name="h_grouped%d" % h, align_bytes=64)
-            nc.scalar.activation(out=h_grouped[:], in_=h_acc[:].rearrange("p t c -> p c t"), func=ACT.Relu)
-            h_codes = keep.tile([P, HALF], U32, name="h_codes%d" % h, align_bytes=64)
-            h_plane = keep.tile([P, HALF], U8, name="h_plane%d" % h, align_bytes=64)
-            nc.vector.quantize_mx(
-                out=h_codes[:].bitcast(FP8X4),
-                scales=h_plane[:],
-                in_=h_grouped[:].rearrange("p c t -> p (c t)"),
-            )
-            for c in range(OUT_TILES):
-                y_acc = psum_y.tile([P, HALF], F32, name="y_acc")
+        def first_product(acc, t, codes, plane):
+            for a in range(PASSES):
                 nc.tensor.matmul_mx(
-                    out=y_acc[:],
+                    out=acc,
+                    lhsT=w1_codes[:, a, t, :].bitcast(FP8X4),
+                    lhsT_scale=w1_plane[:, a, t, :],
+                    rhs=codes[:, a, :].bitcast(FP8X4),
+                    rhs_scale=plane[:, a, :],
+                    start=(a == 0),
+                    stop=(a == PASSES - 1),
+                )
+
+        def quantise_h(h, grouped):
+            codes = keep.tile([P, HALF], U32, name="h_codes%d" % h, align_bytes=64)
+            plane = keep.tile([P, HALF], U8, name="h_plane%d" % h, align_bytes=64)
+            nc.vector.quantize_mx(
+                out=codes[:].bitcast(FP8X4),
+                scales=plane[:],
+                in_=grouped[:].rearrange("p c t -> p (c t)"),
+            )
+            return codes, plane
+
+        acts = {}
+
+        def second_product(h, tiles, acc, codes, plane):
+            for i, c in enumerate(tiles):
+                nc.tensor.matmul_mx(
+                    out=acc[:, i, :],
                     lhsT=w2_codes[:, 2 * P * c : 2 * P * (c + 1)].bitcast(FP4X4),
                     lhsT_scale=w2_plane[:, P * c : P * (c + 1)],
-                    rhs=h_codes[:].bitcast(FP8X4),
-                    rhs_scale=h_plane[:],
+                    rhs=codes[:].bitcast(FP8X4),
+                    rhs_scale=plane[:],
                     start=True,
                     stop=True,
                 )
+            for i, c in enumerate(tiles):
                 act = keep.tile([P, HALF], F32, name="act%d%d" % (h, c))
-                nc.scalar.activation(out=act[:], in_=y_acc[:], func=ACT.Gelu_apprx_tanh, bias=bias[:, c : c + 1])
+                nc.scalar.activation(out=act[:], in_=acc[:, i, :], func=ACT.Gelu_apprx_tanh, bias=bias[:, c : c + 1])
                 acts[(h, c)] = act
+
+        xa_codes, xa_plane = quantise_x(0)
+        ha_low = psum.tile([P, 2, HALF], F32, name="ha_low")
+        ha_high = psum.tile([P, 2, HALF], F32, name="ha_high")
+        for i in range(2):
+            first_product(ha_low[:, i, :], i, xa_codes, xa_plane)
+            first_product(ha_high[:, i, :], 2 + i, xa_codes, xa_plane)
+        ha_grouped = keep.tile([P, HALF, PACK], BF16, name="ha_grouped", align_bytes=64)
+        nc.vector.tensor_scalar_max(ha_grouped[:, :, 0:2], ha_low[:].rearrange("p t c -> p c t"), 0.0)
+        nc.scalar.activation(out=ha_grouped[:, :, 2:4], in_=ha_high[:].rearrange("p t c -> p c t"), func=ACT.Relu)
+        ha_codes, ha_plane = quantise_h(0, ha_grouped)
+        for c in range(2):
+            ya = psum.tile([P, 1, HALF], F32, name="ya%d" % c)
+            second_product(0, [c], ya, ha_codes, ha_plane)
+
+        xb_codes, xb_plane = quantise_x(1)
+        hb = psum.tile([P, PACK, HALF], F32, name="hb", tag="shared_bank")
+        for t in range(PACK):
+            first_product(hb[:, t, :], t, xb_codes, xb_plane)
+        hb_grouped = keep.tile([P, HALF, PACK], BF16, name="hb_grouped", align_bytes=64)
+        nc.scalar.activation(out=hb_grouped[:], in_=hb[:].rearrange("p t c -> p c t"), func=ACT.Relu)
+        hb_codes, hb_plane = quantise_h(1, hb_grouped)
+        ya_late = psum.tile([P, 2, HALF], F32, name="ya_late", tag="shared_bank")
+        second_product(0, [2, 3], ya_late, ha_codes, ha_plane)
+        for c in range(0, OUT_TILES, 2):
+            yb = psum.tile([P, 2, HALF], F32, name="yb%d" % c)
+            second_product(1, [c, c + 1], yb, hb_codes, hb_plane)
 
         for h in range(HALVES):
             list_cols = slice(h * HALF // 16, (h + 1) * HALF // 16)

@@ -25,8 +25,8 @@ HALF = 128
 HALVES = S // HALF
 OUT_TILES = M // P
 
-W1_CHUNKS = [(0, 0, 512, 2), (1, 0, 256, 3), (1, 256, 256, 3)]
-X_ON_VECTOR = {(0, 0): 48, (0, 1): 72, (1, 0): 128, (1, 1): 0}
+W1_CHUNKS = [(0, 0, 256, 2), (0, 256, 256, 2), (1, 0, 256, 2), (1, 256, 256, 2)]
+X_ON_VECTOR = {(0, 0): 32, (0, 1): 64, (1, 0): 128, (1, 1): 64}
 
 
 def tile_list_hscat_m_gelu_kernel(tc, x, w1, w2_words, w2_scales, b, wgo, offs, out):
@@ -37,10 +37,10 @@ def tile_list_hscat_m_gelu_kernel(tc, x, w1, w2_words, w2_scales, b, wgo, offs, 
 
         offsets = keep.tile([P, S // 16], U16, name="offsets")
 
-        w2_plane = keep.tile([P, M], U8, name="w2_plane", align_bytes=64)
-        nc.vector.memset(w2_plane[:].bitcast(I32), 0)
         b_rows = keep.tile([P, P], F32, name="b_rows")
         nc.vector.memset(b_rows[:], 0.0)
+        w2_plane = keep.tile([P, M], U8, name="w2_plane", align_bytes=64)
+        nc.vector.memset(w2_plane[:].bitcast(I32), 0)
         warm_in = keep.tile([P, 1], F32, name="warm_in")
         warm_out = keep.tile([P, 1], F32, name="warm_out")
         nc.vector.memset(warm_in[:], 0.0)
@@ -56,11 +56,6 @@ def tile_list_hscat_m_gelu_kernel(tc, x, w1, w2_words, w2_scales, b, wgo, offs, 
             w1_raw.append(raw)
             if i == 0:
                 nc.sync.dma_start(out=b_rows[0:OUT_TILES, :], in_=b.rearrange("(c p) -> c p", p=P))
-                for q in range(4):
-                    nc.sync.dma_start(
-                        out=w2_plane[32 * q : 32 * q + 4, :].bitcast(I32),
-                        in_=w2_scales[0, 4 * q : 4 * q + 4, :].bitcast(I32),
-                    )
 
         x_raw = {}
 
@@ -74,13 +69,18 @@ def tile_list_hscat_m_gelu_kernel(tc, x, w1, w2_words, w2_scales, b, wgo, offs, 
 
         load_x(0, 0)
         load_x(0, 1)
-        nc.sync.dma_start(offsets[:], offs)
+        load_x(1, 0)
         w2_codes = keep.tile([P, 2 * M], U8, name="w2_codes", align_bytes=64)
         nc.sync.dma_start(out=w2_codes[:].bitcast(I32), in_=w2_words[0].bitcast(I32))
-        load_x(1, 0)
         load_x(1, 1)
+        for q in range(4):
+            nc.sync.dma_start(
+                out=w2_plane[32 * q : 32 * q + 4, :].bitcast(I32),
+                in_=w2_scales[0, 4 * q : 4 * q + 4, :].bitcast(I32),
+            )
         weights = keep.tile([P, S], F32, name="weights")
         nc.sync.dma_start(out=weights[:], in_=wgo)
+        nc.sync.dma_start(offsets[:], offs)
 
         ident = keep.tile([P, P], F32, name="ident")
         make_identity(nc, ident[:])
@@ -88,6 +88,10 @@ def tile_list_hscat_m_gelu_kernel(tc, x, w1, w2_words, w2_scales, b, wgo, offs, 
         nc.tensor.transpose(b_turned[:], b_rows[:], ident[:])
         bias = keep.tile([P, OUT_TILES], F32, name="bias")
         nc.scalar.copy(out=bias[:], in_=b_turned[:, 0:OUT_TILES])
+        idle_bank = psum.tile([P, 4, P], F32, name="idle_bank")
+        for raw in w1_raw[1:]:
+            for i in range(8):
+                nc.tensor.transpose(idle_bank[:, i % 4, :], raw[:, i % 4, P * (i // 4) : P * (i // 4 + 1)], ident[:])
 
         windows = []
         for c in range(OUT_TILES):
@@ -176,6 +180,14 @@ def tile_list_hscat_m_gelu_kernel(tc, x, w1, w2_words, w2_scales, b, wgo, offs, 
                 nc.scalar.activation(out=act[:], in_=acc[:, i, :], func=ACT.Gelu_apprx_tanh, bias=bias[:, c : c + 1])
                 acts[(h, c)] = act
 
+        def scatter(h, c):
+            nc.vector.tensor_tensor(
+                windows[c][:].indirect(offsets[:, h * HALF // 16 : (h + 1) * HALF // 16]),
+                acts[(h, c)][:],
+                weights[:, h * HALF : (h + 1) * HALF],
+                MULT,
+            )
+
         xa_codes, xa_plane = quantise_x(0)
         ha_low = psum.tile([P, 2, HALF], F32, name="ha_low")
         ha_high = psum.tile([P, 2, HALF], F32, name="ha_high")
@@ -184,33 +196,27 @@ def tile_list_hscat_m_gelu_kernel(tc, x, w1, w2_words, w2_scales, b, wgo, offs, 
             first_product(ha_high[:, i, :], 2 + i, xa_codes, xa_plane)
         ha_grouped = keep.tile([P, HALF, PACK], BF16, name="ha_grouped", align_bytes=64)
         nc.vector.tensor_scalar_max(ha_grouped[:, :, 0:2], ha_low[:].rearrange("p t c -> p c t"), 0.0)
-        nc.scalar.activation(out=ha_grouped[:, :, 2:4], in_=ha_high[:].rearrange("p t c -> p c t"), func=ACT.Relu)
+        nc.scalar.activation(out=ha_grouped[:, :, 2:4], in_=ha_high[:].rearrange("p t c -> p c t"), func=ACT.Relu, bias=warm_out[:])
         ha_codes, ha_plane = quantise_h(0, ha_grouped)
-        for c in range(2):
-            ya = psum.tile([P, 1, HALF], F32, name="ya%d" % c)
-            second_product(0, [c], ya, ha_codes, ha_plane)
-
         xb_codes, xb_plane = quantise_x(1)
+        ya_first = psum.tile([P, 1, HALF], F32, name="ya_first", tag="shared_bank")
+        second_product(0, [0], ya_first, ha_codes, ha_plane)
+        ya_next = psum.tile([P, 2, HALF], F32, name="ya_next")
+        second_product(0, [1, 2], ya_next, ha_codes, ha_plane)
+
         hb = psum.tile([P, PACK, HALF], F32, name="hb", tag="shared_bank")
         for t in range(PACK):
             first_product(hb[:, t, :], t, xb_codes, xb_plane)
         hb_grouped = keep.tile([P, HALF, PACK], BF16, name="hb_grouped", align_bytes=64)
         nc.scalar.activation(out=hb_grouped[:], in_=hb[:].rearrange("p t c -> p c t"), func=ACT.Relu)
         hb_codes, hb_plane = quantise_h(1, hb_grouped)
-        ya_late = psum.tile([P, 2, HALF], F32, name="ya_late", tag="shared_bank")
-        second_product(0, [2, 3], ya_late, ha_codes, ha_plane)
+        ya_late = psum.tile([P, 1, HALF], F32, name="ya_late", tag="shared_bank")
+        second_product(0, [3], ya_late, ha_codes, ha_plane)
         for c in range(0, OUT_TILES, 2):
             yb = psum.tile([P, 2, HALF], F32, name="yb%d" % c)
             second_product(1, [c, c + 1], yb, hb_codes, hb_plane)
-
-        for h in range(HALVES):
-            list_cols = slice(h * HALF // 16, (h + 1) * HALF // 16)
-            for c in range(OUT_TILES):
-                nc.vector.tensor_tensor(
-                    windows[c][:].indirect(offsets[:, list_cols]),
-                    acts[(h, c)][:],
-                    weights[:, h * HALF : (h + 1) * HALF],
-                    MULT,
-                )
-                if h == HALVES - 1:
-                    nc.sync.dma_start(out=out[P * c : P * (c + 1), :], in_=windows[c][:])
+        for c in range(OUT_TILES):
+            scatter(0, c)
+        for c in range(OUT_TILES):
+            scatter(1, c)
+            nc.sync.dma_start(out=out[P * c : P * (c + 1), :], in_=windows[c][:])

@@ -88,10 +88,6 @@ def tile_list_hscat_m_gelu_kernel(tc, x, w1, w2_words, w2_scales, b, wgo, offs, 
         nc.tensor.transpose(b_turned[:], b_rows[:], ident[:])
         bias = keep.tile([P, OUT_TILES], F32, name="bias")
         nc.scalar.copy(out=bias[:], in_=b_turned[:, 0:OUT_TILES])
-        idle_bank = psum.tile([P, 4, P], F32, name="idle_bank")
-        for raw in w1_raw[1:]:
-            for i in range(8):
-                nc.tensor.transpose(idle_bank[:, i % 4, :], raw[:, i % 4, P * (i // 4) : P * (i // 4 + 1)], ident[:])
 
         windows = []
         for c in range(OUT_TILES):

@@ -22,11 +22,8 @@ PACK = 4
 K_PASS = P * PACK
 PASSES = K // K_PASS
 HALF = 128
-HALVES = S // HALF
 OUT_TILES = M // P
-
-W1_CHUNKS = [(0, 0, 256, 2), (0, 256, 256, 2), (1, 0, 256, 2), (1, 256, 256, 2)]
-X_ON_VECTOR = {(0, 0): 32, (0, 1): 64, (1, 0): 128, (1, 1): 64}
+X_ON_VECTOR = {(0, 0): 64, (0, 1): 64, (1, 0): 0, (1, 1): 128}
 
 
 def tile_list_hscat_m_gelu_kernel(tc, x, w1, w2_words, w2_scales, b, wgo, offs, out):
@@ -39,25 +36,23 @@ def tile_list_hscat_m_gelu_kernel(tc, x, w1, w2_words, w2_scales, b, wgo, offs, 
 
         b_rows = keep.tile([P, P], F32, name="b_rows")
         nc.vector.memset(b_rows[:], 0.0)
+        zero_in = keep.tile([P, 1], F32, name="zero_in")
+        zero = keep.tile([P, 1], F32, name="zero")
+        nc.vector.memset(zero_in[:], 0.0)
+        nc.scalar.activation(out=zero[:], in_=zero_in[:], func=ACT.Gelu_apprx_tanh)
         w2_plane = keep.tile([P, M], U8, name="w2_plane", align_bytes=64)
         nc.vector.memset(w2_plane[:].bitcast(I32), 0)
-        warm_in = keep.tile([P, 1], F32, name="warm_in")
-        warm_out = keep.tile([P, 1], F32, name="warm_out")
-        nc.vector.memset(warm_in[:], 0.0)
-        nc.scalar.activation(out=warm_out[:], in_=warm_in[:], func=ACT.Gelu_apprx_tanh)
 
-        w1_raw = []
-        for i, (a, c0, cols, on_v) in enumerate(W1_CHUNKS):
-            raw = keep.tile([P, PACK, cols], F32, name="w1_raw%d" % i)
+        w1_raw = {}
+        x_raw = {}
+
+        def load_w1(a, c0, cols):
+            raw = keep.tile([P, PACK, cols], F32, name="w1_raw%d_%d" % (a, c0))
             nc.sync.dma_start(
                 out=raw[:],
                 in_=w1[a * K_PASS : (a + 1) * K_PASS, c0 : c0 + cols].rearrange("(p j) c -> p j c", j=PACK),
             )
-            w1_raw.append(raw)
-            if i == 0:
-                nc.sync.dma_start(out=b_rows[0:OUT_TILES, :], in_=b.rearrange("(c p) -> c p", p=P))
-
-        x_raw = {}
+            w1_raw[(a, c0)] = raw
 
         def load_x(h, a):
             raw = keep.tile([P, PACK, HALF], F32, name="x_raw%d%d" % (h, a))
@@ -67,24 +62,29 @@ def tile_list_hscat_m_gelu_kernel(tc, x, w1, w2_words, w2_scales, b, wgo, offs, 
             )
             x_raw[(h, a)] = raw
 
+        load_w1(0, 0, 512)
+        nc.sync.dma_start(out=b_rows[0:OUT_TILES, :], in_=b.rearrange("(c p) -> c p", p=P))
         load_x(0, 0)
+        load_w1(1, 0, 256)
         load_x(0, 1)
+        load_w1(1, 256, 128)
+        load_w1(1, 384, 128)
         load_x(1, 0)
         w2_codes = keep.tile([P, 2 * M], U8, name="w2_codes", align_bytes=64)
         nc.sync.dma_start(out=w2_codes[:].bitcast(I32), in_=w2_words[0].bitcast(I32))
-        load_x(1, 1)
         for q in range(4):
             nc.sync.dma_start(
                 out=w2_plane[32 * q : 32 * q + 4, :].bitcast(I32),
                 in_=w2_scales[0, 4 * q : 4 * q + 4, :].bitcast(I32),
             )
+        load_x(1, 1)
         weights = keep.tile([P, S], F32, name="weights")
         nc.sync.dma_start(out=weights[:], in_=wgo)
         nc.sync.dma_start(offsets[:], offs)
 
         ident = keep.tile([P, P], F32, name="ident")
         make_identity(nc, ident[:])
-        b_turned = psum.tile([P, P], F32, name="b_turned")
+        b_turned = psum.tile([P, P], F32, name="b_turned", tag="bank_y00")
         nc.tensor.transpose(b_turned[:], b_rows[:], ident[:])
         bias = keep.tile([P, OUT_TILES], F32, name="bias")
         nc.scalar.copy(out=bias[:], in_=b_turned[:, 0:OUT_TILES])
@@ -95,72 +95,73 @@ def tile_list_hscat_m_gelu_kernel(tc, x, w1, w2_words, w2_scales, b, wgo, offs, 
             nc.vector.memset(window[:], 0.0)
             windows.append(window)
 
-        w1_codes = keep.tile([P, PASSES, PACK, P], U32, name="w1_codes", align_bytes=64)
-        w1_plane = keep.tile([P, PASSES, PACK, P], U8, name="w1_plane", align_bytes=64)
-        for i, (a, c0, cols, on_vector) in enumerate(W1_CHUNKS):
-            ms = cols // PACK
-            m0 = c0 // PACK
-            src = w1_raw[i][:].rearrange("p j (m t) -> p m j t", t=PACK)
-            part_v = keep.tile([P, on_vector, ms, PACK], BF16, name="w1_v%d" % i, align_bytes=64)
-            part_s = keep.tile([P, PACK - on_vector, ms, PACK], BF16, name="w1_s%d" % i, align_bytes=64)
-            nc.vector.tensor_copy(out=part_v[:].rearrange("p t m j -> p m j t"), in_=src[:, :, :, 0:on_vector])
-            nc.scalar.copy(out=part_s[:].rearrange("p t m j -> p m j t"), in_=src[:, :, :, on_vector:PACK])
+        w1_codes = {}
+        w1_plane = {}
+        for a in range(PASSES):
             for t in range(PACK):
-                grouped = part_v[:, t] if t < on_vector else part_s[:, t - on_vector]
+                w1_codes[(a, t)] = keep.tile([P, P], U32, name="w1_codes%d%d" % (a, t), align_bytes=64)
+                w1_plane[(a, t)] = keep.tile([P, P], U8, name="w1_plane%d%d" % (a, t), align_bytes=64)
+
+        def quantise_w1(a, pieces):
+            first = pieces[0][0]
+            ms = sum(cols for c0, cols in pieces) // PACK
+            part_v = keep.tile([P, 2, ms, PACK], BF16, name="w1_v%d_%d" % (a, first), align_bytes=64)
+            part_s = keep.tile([P, 2, ms, PACK], BF16, name="w1_s%d_%d" % (a, first), align_bytes=64)
+            for c0, cols in pieces:
+                src = w1_raw[(a, c0)][:].rearrange("p j (m t) -> p m j t", t=PACK)
+                here = slice((c0 - first) // PACK, (c0 - first + cols) // PACK)
+                nc.vector.tensor_copy(out=part_v[:, :, here].rearrange("p t m j -> p m j t"), in_=src[:, :, :, 0:2])
+                nc.scalar.copy(out=part_s[:, :, here].rearrange("p t m j -> p m j t"), in_=src[:, :, :, 2:PACK])
+            m0 = first // PACK
+            for t in range(PACK):
+                grouped = part_v[:, t] if t < 2 else part_s[:, t - 2]
                 nc.vector.quantize_mx(
-                    out=w1_codes[:, a, t, m0 : m0 + ms].bitcast(FP8X4),
-                    scales=w1_plane[:, a, t, m0 : m0 + ms],
+                    out=w1_codes[(a, t)][:, m0 : m0 + ms].bitcast(FP8X4),
+                    scales=w1_plane[(a, t)][:, m0 : m0 + ms],
                     in_=grouped.rearrange("p m j -> p (m j)"),
                 )
 
-        def quantise_x(h):
-            codes = keep.tile([P, PASSES, HALF], U32, name="x_codes%d" % h, tag="late" if h == 0 else "xb_codes", align_bytes=64)
-            plane = keep.tile([P, PASSES, HALF], U8, name="x_plane%d" % h, align_bytes=64)
-            x_grouped = []
-            for a in range(PASSES):
-                name = "x_grouped%d%d" % (h, a)
-                grouped = keep.tile([P, HALF, PACK], BF16, name=name, tag="late" if (h, a) == (1, 1) else name, align_bytes=64)
-                dst = grouped[:].rearrange("p (c i) j -> p c j i", i=4)
-                src = x_raw[(h, a)][:].rearrange("p j (c i) -> p c j i", i=4)
-                cut = X_ON_VECTOR[(h, a)] // 4
-                if cut > 0:
-                    nc.vector.tensor_copy(out=dst[:, 0:cut], in_=src[:, 0:cut])
-                if cut < HALF // 4:
-                    nc.scalar.copy(out=dst[:, cut:], in_=src[:, cut:])
-                x_grouped.append(grouped)
-            for a in range(PASSES):
-                nc.vector.quantize_mx(
-                    out=codes[:, a, :].bitcast(FP8X4),
-                    scales=plane[:, a, :],
-                    in_=x_grouped[a][:].rearrange("p c j -> p (c j)"),
-                )
-            return codes, plane
+        def round_x(h, a, tag):
+            grouped = keep.tile([P, HALF, PACK], BF16, name="x_grouped%d%d" % (h, a), tag=tag, align_bytes=64)
+            dst = grouped[:].rearrange("p (c i) j -> p c j i", i=4)
+            src = x_raw[(h, a)][:].rearrange("p j (c i) -> p c j i", i=4)
+            cut = X_ON_VECTOR[(h, a)] // 4
+            if cut > 0:
+                nc.vector.tensor_copy(out=dst[:, 0:cut], in_=src[:, 0:cut])
+            if cut < HALF // 4:
+                nc.scalar.copy(out=dst[:, cut:], in_=src[:, cut:])
+            return grouped
 
-        def first_product(acc, t, codes, plane):
-            for a in range(PASSES):
-                nc.tensor.matmul_mx(
-                    out=acc,
-                    lhsT=w1_codes[:, a, t, :].bitcast(FP8X4),
-                    lhsT_scale=w1_plane[:, a, t, :],
-                    rhs=codes[:, a, :].bitcast(FP8X4),
-                    rhs_scale=plane[:, a, :],
-                    start=(a == 0),
-                    stop=(a == PASSES - 1),
-                )
-
-        def quantise_h(h, grouped):
-            codes = keep.tile([P, HALF], U32, name="h_codes%d" % h, align_bytes=64)
-            plane = keep.tile([P, HALF], U8, name="h_plane%d" % h, align_bytes=64)
+        def quantise(name, grouped, tag):
+            codes = keep.tile([P, HALF], U32, name=name + "_codes", tag=tag, align_bytes=64)
+            plane = keep.tile([P, HALF], U8, name=name + "_plane", align_bytes=64)
             nc.vector.quantize_mx(
                 out=codes[:].bitcast(FP8X4),
                 scales=plane[:],
-                in_=grouped[:].rearrange("p c t -> p (c t)"),
+                in_=grouped[:].rearrange("p c j -> p (c j)"),
             )
             return codes, plane
 
+        def first_product(banks, a, operand):
+            codes, plane = operand
+            per_bank = PACK // len(banks)
+            for t in range(PACK):
+                nc.tensor.matmul_mx(
+                    out=banks[t // per_bank][:, t % per_bank, :],
+                    lhsT=w1_codes[(a, t)][:].bitcast(FP8X4),
+                    lhsT_scale=w1_plane[(a, t)][:],
+                    rhs=codes[:].bitcast(FP8X4),
+                    rhs_scale=plane[:],
+                    start=(a == 0 and t % per_bank == 0),
+                    stop=(a == PASSES - 1 and t % per_bank == per_bank - 1),
+                )
+
         acts = {}
 
-        def second_product(h, tiles, acc, codes, plane):
+        def second_product(h, tiles, operand, bank_tag, act_tag):
+            codes, plane = operand
+            acc = psum.tile([P, len(tiles), HALF], F32, name="y%d%d" % (h, tiles[0]), tag=bank_tag)
+            act = keep.tile([P, len(tiles), HALF], F32, name="act%d%d" % (h, tiles[0]), tag=act_tag, align_bytes=64)
             for i, c in enumerate(tiles):
                 nc.tensor.matmul_mx(
                     out=acc[:, i, :],
@@ -172,45 +173,43 @@ def tile_list_hscat_m_gelu_kernel(tc, x, w1, w2_words, w2_scales, b, wgo, offs, 
                     stop=True,
                 )
             for i, c in enumerate(tiles):
-                act = keep.tile([P, HALF], F32, name="act%d%d" % (h, c))
-                nc.scalar.activation(out=act[:], in_=acc[:, i, :], func=ACT.Gelu_apprx_tanh, bias=bias[:, c : c + 1])
-                acts[(h, c)] = act
+                nc.scalar.activation(out=act[:, i, :], in_=acc[:, i, :], func=ACT.Gelu_apprx_tanh, bias=bias[:, c : c + 1])
+                acts[(h, c)] = act[:, i, :]
 
         def scatter(h, c):
             nc.vector.tensor_tensor(
                 windows[c][:].indirect(offsets[:, h * HALF // 16 : (h + 1) * HALF // 16]),
-                acts[(h, c)][:],
+                acts[(h, c)],
                 weights[:, h * HALF : (h + 1) * HALF],
                 MULT,
             )
 
-        xa_codes, xa_plane = quantise_x(0)
         ha_low = psum.tile([P, 2, HALF], F32, name="ha_low")
         ha_high = psum.tile([P, 2, HALF], F32, name="ha_high")
-        for i in range(2):
-            first_product(ha_low[:, i, :], i, xa_codes, xa_plane)
-            first_product(ha_high[:, i, :], 2 + i, xa_codes, xa_plane)
+        hb = psum.tile([P, PACK, HALF], F32, name="hb")
+        quantise_w1(0, [(0, 512)])
+        xa0 = quantise("xa0", round_x(0, 0, "xa0_rounded"), "xa0_codes")
+        first_product([ha_low, ha_high], 0, xa0)
+        quantise_w1(1, [(0, 256)])
+        xa1 = quantise("xa1", round_x(0, 1, "xa1_rounded"), "xa1_codes")
+        quantise_w1(1, [(256, 128), (384, 128)])
+        first_product([ha_low, ha_high], 1, xa1)
+        xb0 = quantise("xb0", round_x(1, 0, "xb0_rounded"), "xb0_codes")
         ha_grouped = keep.tile([P, HALF, PACK], BF16, name="ha_grouped", align_bytes=64)
         nc.vector.tensor_scalar_max(ha_grouped[:, :, 0:2], ha_low[:].rearrange("p t c -> p c t"), 0.0)
-        nc.scalar.activation(out=ha_grouped[:, :, 2:4], in_=ha_high[:].rearrange("p t c -> p c t"), func=ACT.Relu, bias=warm_out[:])
-        ha_codes, ha_plane = quantise_h(0, ha_grouped)
-        xb_codes, xb_plane = quantise_x(1)
-        ya_first = psum.tile([P, 1, HALF], F32, name="ya_first", tag="shared_bank")
-        second_product(0, [0], ya_first, ha_codes, ha_plane)
-        ya_next = psum.tile([P, 2, HALF], F32, name="ya_next")
-        second_product(0, [1, 2], ya_next, ha_codes, ha_plane)
-
-        hb = psum.tile([P, PACK, HALF], F32, name="hb", tag="shared_bank")
-        for t in range(PACK):
-            first_product(hb[:, t, :], t, xb_codes, xb_plane)
+        nc.scalar.activation(out=ha_grouped[:, :, 2:4], in_=ha_high[:].rearrange("p t c -> p c t"), func=ACT.Relu, bias=zero[:])
+        ha = quantise("ha", ha_grouped, "ha_codes")
+        second_product(0, [0], ha, "bank_y00", "act00")
+        xb1 = quantise("xb1", round_x(1, 1, "xb1_rounded"), "after_second_half")
+        second_product(0, [1], ha, "bank_y01", "act01")
+        first_product([hb], 0, xb0)
+        first_product([hb], 1, xb1)
         hb_grouped = keep.tile([P, HALF, PACK], BF16, name="hb_grouped", align_bytes=64)
         nc.scalar.activation(out=hb_grouped[:], in_=hb[:].rearrange("p t c -> p c t"), func=ACT.Relu)
-        hb_codes, hb_plane = quantise_h(1, hb_grouped)
-        ya_late = psum.tile([P, 1, HALF], F32, name="ya_late", tag="shared_bank")
-        second_product(0, [3], ya_late, ha_codes, ha_plane)
-        for c in range(0, OUT_TILES, 2):
-            yb = psum.tile([P, 2, HALF], F32, name="yb%d" % c)
-            second_product(1, [c, c + 1], yb, hb_codes, hb_plane)
+        hb_operand = quantise("hb", hb_grouped, "act01")
+        second_product(0, [2, 3], ha, "bank_y02", "after_second_half")
+        second_product(1, [0], hb_operand, "bank_y10", "act10")
+        second_product(1, [1, 2, 3], hb_operand, "bank_y11", "act11")
         for c in range(OUT_TILES):
             scatter(0, c)
         for c in range(OUT_TILES):

@@ -206,11 +206,13 @@ def tile_list_hscat_m_gelu_kernel(tc, x, w1, w2_words, w2_scales, b, wgo, offs, 
         first_product([hb], 1, xb1)
         hb_grouped = keep.tile([P, HALF, PACK], BF16, name="hb_grouped", align_bytes=64)
         nc.scalar.activation(out=hb_grouped[:], in_=hb[:].rearrange("p t c -> p c t"), func=ACT.Relu)
-        hb_operand = quantise("hb", hb_grouped, "act01")
+        scatter(0, 0)
+        scatter(0, 1)
+        hb_operand = quantise("hb", hb_grouped, "act00")
         second_product(0, [2, 3], ha, "bank_y02", "after_second_half")
         second_product(1, [0], hb_operand, "bank_y10", "act10")
         second_product(1, [1, 2, 3], hb_operand, "bank_y11", "act11")
-        for c in range(OUT_TILES):
+        for c in range(2, OUT_TILES):
             scatter(0, c)
         for c in range(OUT_TILES):
             scatter(1, c)

@@ -23,7 +23,7 @@ K_PASS = P * PACK
 PASSES = K // K_PASS
 HALF = 128
 OUT_TILES = M // P
-X_ON_VECTOR = {(0, 0): 64, (0, 1): 64, (1, 0): 0, (1, 1): 128}
+X_ON_VECTOR = {(0, 0): 64, (0, 1): 32, (1, 0): 0, (1, 1): 128}
 
 
 def tile_list_hscat_m_gelu_kernel(tc, x, w1, w2_words, w2_scales, b, wgo, offs, out):
@@ -62,12 +62,13 @@ def tile_list_hscat_m_gelu_kernel(tc, x, w1, w2_words, w2_scales, b, wgo, offs, 
             )
             x_raw[(h, a)] = raw
 
-        load_w1(0, 0, 512)
+        load_w1(0, 0, 256)
+        load_w1(0, 256, 256)
         nc.sync.dma_start(out=b_rows[0:OUT_TILES, :], in_=b.rearrange("(c p) -> c p", p=P))
         load_x(0, 0)
         load_w1(1, 0, 256)
-        load_x(0, 1)
         load_w1(1, 256, 128)
+        load_x(0, 1)
         load_w1(1, 384, 128)
         load_x(1, 0)
         w2_codes = keep.tile([P, 2 * M], U8, name="w2_codes", align_bytes=64)
@@ -187,12 +188,14 @@ def tile_list_hscat_m_gelu_kernel(tc, x, w1, w2_words, w2_scales, b, wgo, offs, 
         ha_low = psum.tile([P, 2, HALF], F32, name="ha_low")
         ha_high = psum.tile([P, 2, HALF], F32, name="ha_high")
         hb = psum.tile([P, PACK, HALF], F32, name="hb")
-        quantise_w1(0, [(0, 512)])
+        quantise_w1(0, [(0, 256)])
+        quantise_w1(0, [(256, 256)])
         xa0 = quantise("xa0", round_x(0, 0, "xa0_rounded"), "xa0_codes")
         first_product([ha_low, ha_high], 0, xa0)
         quantise_w1(1, [(0, 256)])
+        quantise_w1(1, [(256, 128)])
         xa1 = quantise("xa1", round_x(0, 1, "xa1_rounded"), "xa1_codes")
-        quantise_w1(1, [(256, 128), (384, 128)])
+        quantise_w1(1, [(384, 128)])
         first_product([ha_low, ha_high], 1, xa1)
         xb0 = quantise("xb0", round_x(1, 0, "xb0_rounded"), "xb0_codes")
         ha_grouped = keep.tile([P, HALF, PACK], BF16, name="ha_grouped", align_bytes=64)

@@ -1,7 +1,6 @@
 from contextlib import ExitStack
 
 import concourse.mybir as mybir
-from concourse.masks import make_identity
 
 K, R, M, T, S = 1024, 512, 512, 512, 256
 FLOPS = 2 * K * R * S + 2 * R * M * S
@@ -34,7 +33,7 @@ def tile_list_hscat_m_gelu_kernel(tc, x, w1, w2_words, w2_scales, b, wgo, offs, 
 
         offsets = keep.tile([P, S // 16], U16, name="offsets")
 
-        b_rows = keep.tile([P, P], F32, name="b_rows")
+        b_rows = keep.tile([P, P], F32, name="b_rows", align_bytes=64)
         nc.vector.memset(b_rows[:], 0.0)
         zero_in = keep.tile([P, 1], F32, name="zero_in")
         zero = keep.tile([P, 1], F32, name="zero")
@@ -64,7 +63,10 @@ def tile_list_hscat_m_gelu_kernel(tc, x, w1, w2_words, w2_scales, b, wgo, offs, 
 
         load_w1(0, 0, 256)
         load_w1(0, 256, 256)
-        nc.sync.dma_start(out=b_rows[0:OUT_TILES, :], in_=b.rearrange("(c p) -> c p", p=P))
+        nc.sync.dma_start(
+            out=b_rows[0:P:32, :].rearrange("q (c i) -> q c i", i=32),
+            in_=b.rearrange("(c q i) -> q c i", c=OUT_TILES, i=32),
+        )
         load_x(0, 0)
         load_w1(1, 0, 256)
         load_w1(1, 256, 128)
@@ -83,12 +85,8 @@ def tile_list_hscat_m_gelu_kernel(tc, x, w1, w2_words, w2_scales, b, wgo, offs, 
         nc.sync.dma_start(out=weights[:], in_=wgo)
         nc.sync.dma_start(offsets[:], offs)
 
-        ident = keep.tile([P, P], F32, name="ident")
-        make_identity(nc, ident[:])
-        b_turned = psum.tile([P, P], F32, name="b_turned", tag="bank_y00")
-        nc.tensor.transpose(b_turned[:], b_rows[:], ident[:])
-        bias = keep.tile([P, OUT_TILES], F32, name="bias")
-        nc.scalar.copy(out=bias[:], in_=b_turned[:, 0:OUT_TILES])
+        bias = keep.tile([P, P], F32, name="bias", align_bytes=64)
+        nc.vector.transpose(bias[:], b_rows[:])
 
         windows = []
         for c in range(OUT_TILES):
@@ -174,7 +172,7 @@ def tile_list_hscat_m_gelu_kernel(tc, x, w1, w2_words, w2_scales, b, wgo, offs, 
                     stop=True,
                 )
             for i, c in enumerate(tiles):
-                nc.scalar.activation(out=act[:, i, :], in_=acc[:, i, :], func=ACT.Gelu_apprx_tanh, bias=bias[:, c : c + 1])
+                nc.scalar.activation(out=act[:, i, :], in_=acc[:, i, :], func=ACT.Gelu_apprx_tanh, bias=bias[:, 32 * c : 32 * c + 1])
                 acts[(h, c)] = act[:, i, :]
 
         def scatter(h, c):

@@ -36,9 +36,7 @@ def tile_list_hscat_m_gelu_kernel(tc, x, w1, w2_words, w2_scales, b, wgo, offs, 
         b_rows = keep.tile([P, P], F32, name="b_rows", align_bytes=64)
         nc.vector.memset(b_rows[:], 0.0)
         zero_in = keep.tile([P, 1], F32, name="zero_in")
-        zero = keep.tile([P, 1], F32, name="zero")
         nc.vector.memset(zero_in[:], 0.0)
-        nc.scalar.activation(out=zero[:], in_=zero_in[:], func=ACT.Gelu_apprx_tanh)
         w2_plane = keep.tile([P, M], U8, name="w2_plane", align_bytes=64)
         nc.vector.memset(w2_plane[:].bitcast(I32), 0)
 
@@ -86,6 +84,8 @@ def tile_list_hscat_m_gelu_kernel(tc, x, w1, w2_words, w2_scales, b, wgo, offs, 
         nc.sync.dma_start(offsets[:], offs)
 
         bias = keep.tile([P, P], F32, name="bias", align_bytes=64)
+        zero = keep.tile([P, 1], F32, name="zero")
+        nc.scalar.activation(out=zero[:], in_=zero_in[:], func=ACT.Gelu_apprx_tanh)
         nc.vector.transpose(bias[:], b_rows[:])
 
         windows = []

@@ -22,6 +22,8 @@ K_PASS = P * PACK
 PASSES = K // K_PASS
 HALF = 128
 OUT_TILES = M // P
+ROW = 4 * HALF
+ACT_AT = 4 * S + 128
 X_ON_VECTOR = {(0, 0): 64, (0, 1): 32, (1, 0): 0, (1, 1): 128}
 
 
@@ -30,6 +32,12 @@ def tile_list_hscat_m_gelu_kernel(tc, x, w1, w2_words, w2_scales, b, wgo, offs, 
     with ExitStack() as ctx:
         keep = ctx.enter_context(tc.tile_pool(name="keep", bufs=1))
         psum = ctx.enter_context(tc.psum_pool(name="psum", bufs=1))
+        placed = ctx.enter_context(tc.tile_pool(name="placed", bufs=1))
+
+        def place(shape, dtype, name, where):
+            if isinstance(where, int):
+                return placed.tile(shape, dtype, name=name, align_bytes=64, offset=where)
+            return keep.tile(shape, dtype, name=name, tag=where, align_bytes=64)
 
         offsets = keep.tile([P, S // 16], U16, name="offsets")
 
@@ -79,7 +87,7 @@ def tile_list_hscat_m_gelu_kernel(tc, x, w1, w2_words, w2_scales, b, wgo, offs, 
                 in_=w2_scales[0, 4 * q : 4 * q + 4, :].bitcast(I32),
             )
         load_x(1, 1)
-        weights = keep.tile([P, S], F32, name="weights")
+        weights = place([P, S], F32, "weights", 0)
         nc.sync.dma_start(out=weights[:], in_=wgo)
         nc.sync.dma_start(offsets[:], offs)
 
@@ -132,7 +140,7 @@ def tile_list_hscat_m_gelu_kernel(tc, x, w1, w2_words, w2_scales, b, wgo, offs, 
             return grouped
 
         def quantise(name, grouped, tag):
-            codes = keep.tile([P, HALF], U32, name=name + "_codes", tag=tag, align_bytes=64)
+            codes = place([P, HALF], U32, name + "_codes", tag)
             plane = keep.tile([P, HALF], U8, name=name + "_plane", align_bytes=64)
             nc.vector.quantize_mx(
                 out=codes[:].bitcast(FP8X4),
@@ -160,7 +168,7 @@ def tile_list_hscat_m_gelu_kernel(tc, x, w1, w2_words, w2_scales, b, wgo, offs, 
         def second_product(h, tiles, operand, bank_tag, act_tag):
             codes, plane = operand
             acc = psum.tile([P, len(tiles), HALF], F32, name="y%d%d" % (h, tiles[0]), tag=bank_tag)
-            act = keep.tile([P, len(tiles), HALF], F32, name="act%d%d" % (h, tiles[0]), tag=act_tag, align_bytes=64)
+            act = place([P, len(tiles), HALF], F32, "act%d%d" % (h, tiles[0]), act_tag)
             for i, c in enumerate(tiles):
                 nc.tensor.matmul_mx(
                     out=acc[:, i, :],
@@ -200,19 +208,19 @@ def tile_list_hscat_m_gelu_kernel(tc, x, w1, w2_words, w2_scales, b, wgo, offs, 
         nc.vector.tensor_scalar_max(ha_grouped[:, :, 0:2], ha_low[:].rearrange("p t c -> p c t"), 0.0)
         nc.scalar.activation(out=ha_grouped[:, :, 2:4], in_=ha_high[:].rearrange("p t c -> p c t"), func=ACT.Relu, bias=zero[:])
         ha = quantise("ha", ha_grouped, "ha_codes")
-        second_product(0, [0], ha, "bank_y00", "act00")
-        xb1 = quantise("xb1", round_x(1, 1, "xb1_rounded"), "after_second_half")
-        second_product(0, [1], ha, "bank_y01", "act01")
+        second_product(0, [0], ha, "bank_y00", ACT_AT)
+        xb1 = quantise("xb1", round_x(1, 1, "xb1_rounded"), ACT_AT + 2 * ROW)
+        second_product(0, [1], ha, "bank_y01", ACT_AT + ROW)
         first_product([hb], 0, xb0)
         first_product([hb], 1, xb1)
         hb_grouped = keep.tile([P, HALF, PACK], BF16, name="hb_grouped", align_bytes=64)
         nc.scalar.activation(out=hb_grouped[:], in_=hb[:].rearrange("p t c -> p c t"), func=ACT.Relu)
         scatter(0, 0)
         scatter(0, 1)
-        hb_operand = quantise("hb", hb_grouped, "act00")
-        second_product(0, [2, 3], ha, "bank_y02", "after_second_half")
-        second_product(1, [0], hb_operand, "bank_y10", "act10")
-        second_product(1, [1, 2, 3], hb_operand, "bank_y11", "act11")
+        hb_operand = quantise("hb", hb_grouped, ACT_AT)
+        second_product(0, [2, 3], ha, "bank_y02", ACT_AT + 2 * ROW)
+        second_product(1, [0], hb_operand, "bank_y10", ACT_AT + 4 * ROW)
+        second_product(1, [1, 2, 3], hb_operand, "bank_y11", ACT_AT + 5 * ROW)
         for c in range(2, OUT_TILES):
             scatter(0, c)
         for c in range(OUT_TILES):

@@ -23,8 +23,8 @@ PASSES = K // K_PASS
 HALF = 128
 OUT_TILES = M // P
 ROW = 4 * HALF
-ACT_AT = 4 * S + 128
-X_ON_VECTOR = {(0, 0): 64, (0, 1): 32, (1, 0): 0, (1, 1): 128}
+ACT_AT = 4 * S + 64
+X_ON_VECTOR = {(0, 0): 64, (0, 1): 32, (1, 0): 64, (1, 1): 128}
 
 
 def tile_list_hscat_m_gelu_kernel(tc, x, w1, w2_words, w2_scales, b, wgo, offs, out):
@@ -33,6 +33,7 @@ def tile_list_hscat_m_gelu_kernel(tc, x, w1, w2_words, w2_scales, b, wgo, offs, 
         keep = ctx.enter_context(tc.tile_pool(name="keep", bufs=1))
         psum = ctx.enter_context(tc.psum_pool(name="psum", bufs=1))
         placed = ctx.enter_context(tc.tile_pool(name="placed", bufs=1))
+        landed = ctx.enter_context(tc.tile_pool(name="landed", bufs=1))
 
         def place(shape, dtype, name, where):
             if isinstance(where, int):
@@ -52,7 +53,7 @@ def tile_list_hscat_m_gelu_kernel(tc, x, w1, w2_words, w2_scales, b, wgo, offs, 
         x_raw = {}
 
         def load_w1(a, c0, cols):
-            raw = keep.tile([P, PACK, cols], F32, name="w1_raw%d_%d" % (a, c0))
+            raw = landed.tile([P, PACK, cols], F32, name="w1_raw%d_%d" % (a, c0), align_bytes=256)
             nc.sync.dma_start(
                 out=raw[:],
                 in_=w1[a * K_PASS : (a + 1) * K_PASS, c0 : c0 + cols].rearrange("(p j) c -> p j c", j=PACK),
@@ -60,7 +61,7 @@ def tile_list_hscat_m_gelu_kernel(tc, x, w1, w2_words, w2_scales, b, wgo, offs, 
             w1_raw[(a, c0)] = raw
 
         def load_x(h, a):
-            raw = keep.tile([P, PACK, HALF], F32, name="x_raw%d%d" % (h, a))
+            raw = landed.tile([P, PACK, HALF], F32, name="x_raw%d%d" % (h, a), align_bytes=256)
             nc.sync.dma_start(
                 out=raw[:],
                 in_=x[a * K_PASS : (a + 1) * K_PASS, h * HALF : (h + 1) * HALF].rearrange("(p j) c -> p j c", j=PACK),
@@ -79,7 +80,7 @@ def tile_list_hscat_m_gelu_kernel(tc, x, w1, w2_words, w2_scales, b, wgo, offs, 
         load_x(0, 1)
         load_w1(1, 384, 128)
         load_x(1, 0)
-        w2_codes = keep.tile([P, 2 * M], U8, name="w2_codes", align_bytes=64)
+        w2_codes = landed.tile([P, 2 * M], U8, name="w2_codes", align_bytes=256)
         nc.sync.dma_start(out=w2_codes[:].bitcast(I32), in_=w2_words[0].bitcast(I32))
         for q in range(4):
             nc.sync.dma_start(
@@ -87,7 +88,7 @@ def tile_list_hscat_m_gelu_kernel(tc, x, w1, w2_words, w2_scales, b, wgo, offs, 
                 in_=w2_scales[0, 4 * q : 4 * q + 4, :].bitcast(I32),
             )
         load_x(1, 1)
-        weights = place([P, S], F32, "weights", 0)
+        weights = placed.tile([P, S], F32, name="weights", align_bytes=256, offset=0)
         nc.sync.dma_start(out=weights[:], in_=wgo)
         nc.sync.dma_start(offsets[:], offs)
 
@@ -206,8 +207,18 @@ def tile_list_hscat_m_gelu_kernel(tc, x, w1, w2_words, w2_scales, b, wgo, offs, 
         xb0 = quantise("xb0", round_x(1, 0, "xb0_rounded"), "xb0_codes")
         ha_grouped = keep.tile([P, HALF, PACK], BF16, name="ha_grouped", align_bytes=64)
         nc.vector.tensor_scalar_max(ha_grouped[:, :, 0:2], ha_low[:].rearrange("p t c -> p c t"), 0.0)
-        nc.scalar.activation(out=ha_grouped[:, :, 2:4], in_=ha_high[:].rearrange("p t c -> p c t"), func=ACT.Relu, bias=zero[:])
-        ha = quantise("ha", ha_grouped, "ha_codes")
+        ha_codes = keep.tile([P, HALF], U32, name="ha_codes", align_bytes=64)
+        ha_plane = keep.tile([P, HALF], U8, name="ha_plane", align_bytes=64)
+        for step in (slice(0, HALF // 2), slice(HALF // 2, HALF)):
+            nc.scalar.activation(
+                out=ha_grouped[:, step, 2:4], in_=ha_high[:, :, step].rearrange("p t c -> p c t"), func=ACT.Relu, bias=zero[:]
+            )
+            nc.vector.quantize_mx(
+                out=ha_codes[:, step].bitcast(FP8X4),
+                scales=ha_plane[:, step],
+                in_=ha_grouped[:, step].rearrange("p c j -> p (c j)"),
+            )
+        ha = (ha_codes, ha_plane)
         second_product(0, [0], ha, "bank_y00", ACT_AT)
         xb1 = quantise("xb1", round_x(1, 1, "xb1_rounded"), ACT_AT + 2 * ROW)
         second_product(0, [1], ha, "bank_y01", ACT_AT + ROW)

@@ -24,7 +24,7 @@ HALF = 128
 OUT_TILES = M // P
 ROW = 4 * HALF
 ACT_AT = 4 * S + 64
-X_ON_VECTOR = {(0, 0): 64, (0, 1): 32, (1, 0): 64, (1, 1): 128}
+X_ON_VECTOR = {(0, 0): 64, (0, 1): 32, (1, 0): 64, (1, 1): 64}
 
 
 def tile_list_hscat_m_gelu_kernel(tc, x, w1, w2_words, w2_scales, b, wgo, offs, out):
@@ -41,6 +41,7 @@ def tile_list_hscat_m_gelu_kernel(tc, x, w1, w2_words, w2_scales, b, wgo, offs, 
             return keep.tile(shape, dtype, name=name, tag=where, align_bytes=64)
 
         offsets = keep.tile([P, S // 16], U16, name="offsets")
+        windows = [keep.tile([P, T], F32, name="window%d" % c) for c in range(OUT_TILES)]
 
         b_rows = keep.tile([P, P], F32, name="b_rows", align_bytes=64)
         nc.vector.memset(b_rows[:], 0.0)
@@ -80,14 +81,14 @@ def tile_list_hscat_m_gelu_kernel(tc, x, w1, w2_words, w2_scales, b, wgo, offs, 
         load_x(0, 1)
         load_w1(1, 384, 128)
         load_x(1, 0)
-        w2_codes = landed.tile([P, 2 * M], U8, name="w2_codes", align_bytes=256)
-        nc.sync.dma_start(out=w2_codes[:].bitcast(I32), in_=w2_words[0].bitcast(I32))
         for q in range(4):
             nc.sync.dma_start(
                 out=w2_plane[32 * q : 32 * q + 4, :].bitcast(I32),
                 in_=w2_scales[0, 4 * q : 4 * q + 4, :].bitcast(I32),
             )
         load_x(1, 1)
+        w2_codes = landed.tile([P, 2 * M], U8, name="w2_codes", align_bytes=256)
+        nc.sync.dma_start(out=w2_codes[:].bitcast(I32), in_=w2_words[0].bitcast(I32))
         weights = placed.tile([P, S], F32, name="weights", align_bytes=256, offset=0)
         nc.sync.dma_start(out=weights[:], in_=wgo)
         nc.sync.dma_start(offsets[:], offs)
@@ -97,11 +98,8 @@ def tile_list_hscat_m_gelu_kernel(tc, x, w1, w2_words, w2_scales, b, wgo, offs, 
         nc.scalar.activation(out=zero[:], in_=zero_in[:], func=ACT.Gelu_apprx_tanh)
         nc.vector.transpose(bias[:], b_rows[:])
 
-        windows = []
-        for c in range(OUT_TILES):
-            window = keep.tile([P, T], F32, name="window%d" % c)
+        for window in windows:
             nc.vector.memset(window[:], 0.0)
-            windows.append(window)
 
         w1_codes = {}
         w1_plane = {}

@@ -87,11 +87,16 @@ def tile_list_hscat_m_gelu_kernel(tc, x, w1, w2_words, w2_scales, b, wgo, offs, 
                 in_=w2_scales[0, 4 * q : 4 * q + 4, :].bitcast(I32),
             )
         load_x(1, 1)
-        w2_codes = landed.tile([P, 2 * M], U8, name="w2_codes", align_bytes=256)
-        nc.sync.dma_start(out=w2_codes[:].bitcast(I32), in_=w2_words[0].bitcast(I32))
-        weights = placed.tile([P, S], F32, name="weights", align_bytes=256, offset=0)
-        nc.sync.dma_start(out=weights[:], in_=wgo)
+        w2_codes = [landed.tile([P, M], U8, name="w2_codes%d" % h, align_bytes=256) for h in range(2)]
+        weights = [placed.tile([P, HALF], F32, name="weights%d" % h, align_bytes=256, offset=h * ROW) for h in range(2)]
+
+        def load_second(h):
+            nc.sync.dma_start(out=w2_codes[h][:].bitcast(I32), in_=w2_words[0, :, h * M : (h + 1) * M].bitcast(I32))
+            nc.sync.dma_start(out=weights[h][:], in_=wgo[:, h * HALF : (h + 1) * HALF])
+
+        load_second(0)
         nc.sync.dma_start(offsets[:], offs)
+        load_second(1)
 
         bias = keep.tile([P, P], F32, name="bias", align_bytes=64)
         zero = keep.tile([P, 1], F32, name="zero")
@@ -171,7 +176,7 @@ def tile_list_hscat_m_gelu_kernel(tc, x, w1, w2_words, w2_scales, b, wgo, offs, 
             for i, c in enumerate(tiles):
                 nc.tensor.matmul_mx(
                     out=acc[:, i, :],
-                    lhsT=w2_codes[:, 2 * P * c : 2 * P * (c + 1)].bitcast(FP4X4),
+                    lhsT=w2_codes[c // 2][:, 2 * P * (c % 2) : 2 * P * (c % 2 + 1)].bitcast(FP4X4),
                     lhsT_scale=w2_plane[:, P * c : P * (c + 1)],
                     rhs=codes[:].bitcast(FP8X4),
                     rhs_scale=plane[:],
@@ -186,7 +191,7 @@ def tile_list_hscat_m_gelu_kernel(tc, x, w1, w2_words, w2_scales, b, wgo, offs, 
             nc.vector.tensor_tensor(
                 windows[c][:].indirect(offsets[:, h * HALF // 16 : (h + 1) * HALF // 16]),
                 acts[(h, c)],
-                weights[:, h * HALF : (h + 1) * HALF],
+                weights[h][:],
                 MULT,
             )
 

@@ -24,6 +24,7 @@ HALF = 128
 OUT_TILES = M // P
 ROW = 4 * HALF
 ACT_AT = 4 * S + 64
+WARM_PASSES, WARM_ROWS = 2, 32
 X_ON_VECTOR = {(0, 0): 64, (0, 1): 32, (1, 0): 64, (1, 1): 64}
 
 
@@ -69,13 +70,13 @@ def tile_list_hscat_m_gelu_kernel(tc, x, w1, w2_words, w2_scales, b, wgo, offs, 
             )
             x_raw[(h, a)] = raw
 
+        load_x(0, 0)
         load_w1(0, 0, 256)
         load_w1(0, 256, 256)
         nc.sync.dma_start(
             out=b_rows[0:P:32, :].rearrange("q (c i) -> q c i", i=32),
             in_=b.rearrange("(c q i) -> q c i", c=OUT_TILES, i=32),
         )
-        load_x(0, 0)
         load_w1(1, 0, 256)
         load_w1(1, 256, 128)
         load_x(0, 1)
@@ -109,9 +110,8 @@ def tile_list_hscat_m_gelu_kernel(tc, x, w1, w2_words, w2_scales, b, wgo, offs, 
         w1_codes = {}
         w1_plane = {}
         for a in range(PASSES):
-            for t in range(PACK):
-                w1_codes[(a, t)] = keep.tile([P, P], U32, name="w1_codes%d%d" % (a, t), align_bytes=64)
-                w1_plane[(a, t)] = keep.tile([P, P], U8, name="w1_plane%d%d" % (a, t), align_bytes=64)
+            w1_codes[a] = keep.tile([P, R], U32, name="w1_codes%d" % a, align_bytes=64)
+            w1_plane[a] = keep.tile([P, R], U8, name="w1_plane%d" % a, align_bytes=64)
 
         def quantise_w1(a, pieces):
             first = pieces[0][0]
@@ -127,8 +127,8 @@ def tile_list_hscat_m_gelu_kernel(tc, x, w1, w2_words, w2_scales, b, wgo, offs, 
             for t in range(PACK):
                 grouped = part_v[:, t] if t < 2 else part_s[:, t - 2]
                 nc.vector.quantize_mx(
-                    out=w1_codes[(a, t)][:, m0 : m0 + ms].bitcast(FP8X4),
-                    scales=w1_plane[(a, t)][:, m0 : m0 + ms],
+                    out=w1_codes[a][:, t * P + m0 : t * P + m0 + ms].bitcast(FP8X4),
+                    scales=w1_plane[a][:, t * P + m0 : t * P + m0 + ms],
                     in_=grouped.rearrange("p m j -> p (m j)"),
                 )
 
@@ -159,8 +159,8 @@ def tile_list_hscat_m_gelu_kernel(tc, x, w1, w2_words, w2_scales, b, wgo, offs, 
             for t in range(PACK):
                 nc.tensor.matmul_mx(
                     out=banks[t // per_bank][:, t % per_bank, :],
-                    lhsT=w1_codes[(a, t)][:].bitcast(FP8X4),
-                    lhsT_scale=w1_plane[(a, t)][:],
+                    lhsT=w1_codes[a][:, t * P : (t + 1) * P].bitcast(FP8X4),
+                    lhsT_scale=w1_plane[a][:, t * P : (t + 1) * P],
                     rhs=codes[:].bitcast(FP8X4),
                     rhs_scale=plane[:],
                     start=(a == 0 and t % per_bank == 0),
@@ -198,9 +198,20 @@ def tile_list_hscat_m_gelu_kernel(tc, x, w1, w2_words, w2_scales, b, wgo, offs, 
         ha_low = psum.tile([P, 2, HALF], F32, name="ha_low")
         ha_high = psum.tile([P, 2, HALF], F32, name="ha_high")
         hb = psum.tile([P, PACK, HALF], F32, name="hb")
+        xa0 = quantise("xa0", round_x(0, 0, "xa0_rounded"), "xa0_codes")
         quantise_w1(0, [(0, 256)])
         quantise_w1(0, [(256, 256)])
-        xa0 = quantise("xa0", round_x(0, 0, "xa0_rounded"), "xa0_codes")
+        unread = psum.tile([WARM_ROWS, R], F32, name="unread", tag="bank_y11")
+        for i in range(WARM_PASSES):
+            nc.tensor.matmul_mx(
+                out=unread[:],
+                lhsT=xa0[0][:, 0:WARM_ROWS].bitcast(FP8X4),
+                lhsT_scale=xa0[1][:, 0:WARM_ROWS],
+                rhs=w1_codes[0][:].bitcast(FP8X4),
+                rhs_scale=w1_plane[0][:],
+                start=True,
+                stop=True,
+            )
         first_product([ha_low, ha_high], 0, xa0)
         quantise_w1(1, [(0, 256)])
         quantise_w1(1, [(256, 128)])

@@ -24,7 +24,7 @@ HALF = 128
 OUT_TILES = M // P
 ROW = 4 * HALF
 ACT_AT = 4 * S + 64
-WARM_PASSES, WARM_ROWS = 2, 32
+WARM_PASSES, WARM_ROWS, WARM_FROM = 2, 32, 64
 X_ON_VECTOR = {(0, 0): 64, (0, 1): 32, (1, 0): 64, (1, 1): 64}
 
 
@@ -109,9 +109,11 @@ def tile_list_hscat_m_gelu_kernel(tc, x, w1, w2_words, w2_scales, b, wgo, offs, 
 
         w1_codes = {}
         w1_plane = {}
+        all_codes = keep.tile([P, PASSES * R], U32, name="w1_codes", align_bytes=64)
+        all_plane = keep.tile([P, PASSES * R], U8, name="w1_plane", align_bytes=64)
         for a in range(PASSES):
-            w1_codes[a] = keep.tile([P, R], U32, name="w1_codes%d" % a, align_bytes=64)
-            w1_plane[a] = keep.tile([P, R], U8, name="w1_plane%d" % a, align_bytes=64)
+            w1_codes[a] = all_codes[:, a * R : (a + 1) * R]
+            w1_plane[a] = all_plane[:, a * R : (a + 1) * R]
 
         def quantise_w1(a, pieces):
             first = pieces[0][0]
@@ -201,19 +203,19 @@ def tile_list_hscat_m_gelu_kernel(tc, x, w1, w2_words, w2_scales, b, wgo, offs, 
         xa0 = quantise("xa0", round_x(0, 0, "xa0_rounded"), "xa0_codes")
         quantise_w1(0, [(0, 256)])
         quantise_w1(0, [(256, 256)])
+        first_product([ha_low, ha_high], 0, xa0)
+        quantise_w1(1, [(0, 256)])
         unread = psum.tile([WARM_ROWS, R], F32, name="unread", tag="bank_y11")
         for i in range(WARM_PASSES):
             nc.tensor.matmul_mx(
                 out=unread[:],
                 lhsT=xa0[0][:, 0:WARM_ROWS].bitcast(FP8X4),
                 lhsT_scale=xa0[1][:, 0:WARM_ROWS],
-                rhs=w1_codes[0][:].bitcast(FP8X4),
-                rhs_scale=w1_plane[0][:],
+                rhs=all_codes[:, WARM_FROM : WARM_FROM + R].bitcast(FP8X4),
+                rhs_scale=all_plane[:, WARM_FROM : WARM_FROM + R],
                 start=True,
                 stop=True,
             )
-        first_product([ha_low, ha_high], 0, xa0)
-        quantise_w1(1, [(0, 256)])
         quantise_w1(1, [(256, 128)])
         xa1 = quantise("xa1", round_x(0, 1, "xa1_rounded"), "xa1_codes")
         quantise_w1(1, [(384, 128)])

@@ -24,7 +24,7 @@ HALF = 128
 OUT_TILES = M // P
 ROW = 4 * HALF
 ACT_AT = 4 * S + 64
-WARM_PASSES, WARM_ROWS, WARM_FROM = 2, 32, 64
+WARM_ROWS = 32
 X_ON_VECTOR = {(0, 0): 64, (0, 1): 32, (1, 0): 64, (1, 1): 64}
 
 
@@ -115,6 +115,20 @@ def tile_list_hscat_m_gelu_kernel(tc, x, w1, w2_words, w2_scales, b, wgo, offs, 
             w1_codes[a] = all_codes[:, a * R : (a + 1) * R]
             w1_plane[a] = all_plane[:, a * R : (a + 1) * R]
 
+        def group(a, t):
+            return (t + a) % PACK * P
+
+        def warm_up(first, cols):
+            nc.tensor.matmul_mx(
+                out=unread[:, 0:cols],
+                lhsT=xa0[0][:, 0:WARM_ROWS].bitcast(FP8X4),
+                lhsT_scale=xa0[1][:, 0:WARM_ROWS],
+                rhs=all_codes[:, first : first + cols].bitcast(FP8X4),
+                rhs_scale=all_plane[:, 0:cols],
+                start=True,
+                stop=True,
+            )
+
         def quantise_w1(a, pieces):
             first = pieces[0][0]
             ms = sum(cols for c0, cols in pieces) // PACK
@@ -129,8 +143,8 @@ def tile_list_hscat_m_gelu_kernel(tc, x, w1, w2_words, w2_scales, b, wgo, offs, 
             for t in range(PACK):
                 grouped = part_v[:, t] if t < 2 else part_s[:, t - 2]
                 nc.vector.quantize_mx(
-                    out=w1_codes[a][:, t * P + m0 : t * P + m0 + ms].bitcast(FP8X4),
-                    scales=w1_plane[a][:, t * P + m0 : t * P + m0 + ms],
+                    out=w1_codes[a][:, group(a, t) + m0 : group(a, t) + m0 + ms].bitcast(FP8X4),
+                    scales=w1_plane[a][:, group(a, t) + m0 : group(a, t) + m0 + ms],
                     in_=grouped.rearrange("p m j -> p (m j)"),
                 )
 
@@ -161,8 +175,8 @@ def tile_list_hscat_m_gelu_kernel(tc, x, w1, w2_words, w2_scales, b, wgo, offs, 
             for t in range(PACK):
                 nc.tensor.matmul_mx(
                     out=banks[t // per_bank][:, t % per_bank, :],
-                    lhsT=w1_codes[a][:, t * P : (t + 1) * P].bitcast(FP8X4),
-                    lhsT_scale=w1_plane[a][:, t * P : (t + 1) * P],
+                    lhsT=w1_codes[a][:, group(a, t) : group(a, t) + P].bitcast(FP8X4),
+                    lhsT_scale=w1_plane[a][:, group(a, t) : group(a, t) + P],
                     rhs=codes[:].bitcast(FP8X4),
                     rhs_scale=plane[:],
                     start=(a == 0 and t % per_bank == 0),
@@ -204,19 +218,12 @@ def tile_list_hscat_m_gelu_kernel(tc, x, w1, w2_words, w2_scales, b, wgo, offs, 
         quantise_w1(0, [(0, 256)])
         quantise_w1(0, [(256, 256)])
         first_product([ha_low, ha_high], 0, xa0)
-        quantise_w1(1, [(0, 256)])
         unread = psum.tile([WARM_ROWS, R], F32, name="unread", tag="bank_y11")
-        for i in range(WARM_PASSES):
-            nc.tensor.matmul_mx(
-                out=unread[:],
-                lhsT=xa0[0][:, 0:WARM_ROWS].bitcast(FP8X4),
-                lhsT_scale=xa0[1][:, 0:WARM_ROWS],
-                rhs=all_codes[:, WARM_FROM : WARM_FROM + R].bitcast(FP8X4),
-                rhs_scale=all_plane[:, WARM_FROM : WARM_FROM + R],
-                start=True,
-                stop=True,
-            )
+        warm_up(0, R)
+        quantise_w1(1, [(0, 256)])
         quantise_w1(1, [(256, 128)])
+        warm_up(96, R)
+        warm_up(R - 32, P)
         xa1 = quantise("xa1", round_x(0, 1, "xa1_rounded"), "xa1_codes")
         quantise_w1(1, [(384, 128)])
         first_product([ha_low, ha_high], 1, xa1)

@@ -45,7 +45,12 @@ def tile_list_hscat_m_gelu_kernel(tc, x, w1, w2_words, w2_scales, b, wgo, offs, 
         windows = [keep.tile([P, T], F32, name="window%d" % c) for c in range(OUT_TILES)]
 
         b_rows = keep.tile([P, P], F32, name="b_rows", align_bytes=64)
-        nc.vector.memset(b_rows[:], 0.0)
+        nc.scalar.dma_start(
+            out=b_rows[31:P:32, :].rearrange("q (c i) -> q c i", i=32),
+            in_=b.rearrange("(c q i) -> q c i", c=OUT_TILES, i=32),
+        )
+        for q in range(4):
+            nc.vector.memset(b_rows[32 * q : 32 * q + 31, :], 0.0)
         zero_in = keep.tile([P, 1], F32, name="zero_in")
         nc.vector.memset(zero_in[:], 0.0)
         w2_plane = keep.tile([P, M], U8, name="w2_plane", align_bytes=64)
@@ -73,10 +78,6 @@ def tile_list_hscat_m_gelu_kernel(tc, x, w1, w2_words, w2_scales, b, wgo, offs, 
         load_x(0, 0)
         load_w1(0, 0, 256)
         load_w1(0, 256, 256)
-        nc.sync.dma_start(
-            out=b_rows[0:P:32, :].rearrange("q (c i) -> q c i", i=32),
-            in_=b.rearrange("(c q i) -> q c i", c=OUT_TILES, i=32),
-        )
         load_w1(1, 0, 256)
         load_w1(1, 256, 128)
         load_x(0, 1)
@@ -200,7 +201,7 @@ def tile_list_hscat_m_gelu_kernel(tc, x, w1, w2_words, w2_scales, b, wgo, offs, 
                     stop=True,
                 )
             for i, c in enumerate(tiles):
-                nc.scalar.activation(out=act[:, i, :], in_=acc[:, i, :], func=ACT.Gelu_apprx_tanh, bias=bias[:, 32 * c : 32 * c + 1])
+                nc.scalar.activation(out=act[:, i, :], in_=acc[:, i, :], func=ACT.Gelu_apprx_tanh, bias=bias[:, 32 * c + 31 : 32 * c + 32])
                 acts[(h, c)] = act[:, i, :]
 
         def scatter(h, c):

@@ -42,7 +42,7 @@ def tile_list_hscat_m_gelu_kernel(tc, x, w1, w2_words, w2_scales, b, wgo, offs, 
             return keep.tile(shape, dtype, name=name, tag=where, align_bytes=64)
 
         offsets = keep.tile([P, S // 16], U16, name="offsets")
-        windows = [keep.tile([P, T], F32, name="window%d" % c) for c in range(OUT_TILES)]
+        windows = [landed.tile([P, T], F32, name="window%d" % c, align_bytes=256) for c in range(OUT_TILES)]
 
         b_rows = keep.tile([P, P], F32, name="b_rows", align_bytes=64)
         nc.scalar.dma_start(

@@ -235,7 +235,7 @@ def tile_list_hscat_m_gelu_kernel(tc, x, w1, w2_words, w2_scales, b, wgo, offs, 
         ha_plane = keep.tile([P, HALF], U8, name="ha_plane", align_bytes=64)
         for step in (slice(0, HALF // 2), slice(HALF // 2, HALF)):
             nc.scalar.activation(
-                out=ha_grouped[:, step, 2:4], in_=ha_high[:, :, step].rearrange("p t c -> p c t"), func=ACT.Relu, bias=zero[:]
+                out=ha_grouped[:, step, 2:4], in_=ha_high[:, :, step].rearrange("p t c -> p c t"), func=ACT.Relu
             )
             nc.vector.quantize_mx(
                 out=ha_codes[:, step].bitcast(FP8X4),
@@ -249,7 +249,7 @@ def tile_list_hscat_m_gelu_kernel(tc, x, w1, w2_words, w2_scales, b, wgo, offs, 
         first_product([hb], 0, xb0)
         first_product([hb], 1, xb1)
         hb_grouped = keep.tile([P, HALF, PACK], BF16, name="hb_grouped", align_bytes=64)
-        nc.scalar.activation(out=hb_grouped[:], in_=hb[:].rearrange("p t c -> p c t"), func=ACT.Relu)
+        nc.scalar.activation(out=hb_grouped[:], in_=hb[:].rearrange("p t c -> p c t"), func=ACT.Relu, bias=zero[:])
         scatter(0, 0)
         scatter(0, 1)
         hb_operand = quantise("hb", hb_grouped, ACT_AT)

from contextlib import ExitStack

import concourse.mybir as mybir

K, R, M, T, S = 1024, 512, 512, 512, 256
FLOPS = 2 * K * R * S + 2 * R * M * S

F32 = mybir.dt.float32
BF16 = mybir.dt.bfloat16
I32 = mybir.dt.int32
U32 = mybir.dt.uint32
U16 = mybir.dt.uint16
U8 = mybir.dt.uint8
FP8X4 = mybir.dt.float8_e4m3fn_x4
FP4X4 = mybir.dt.float4_e2m1fn_x4
ACT = mybir.ActivationFunctionType
MULT = mybir.AluOpType.mult

P = 128
PACK = 4
K_PASS = P * PACK
PASSES = K // K_PASS
HALF = 128
OUT_TILES = M // P
ROW = 4 * HALF
ACT_AT = 4 * S + 64
WARM_ROWS = 32
X_ON_VECTOR = {(0, 0): 64, (0, 1): 32, (1, 0): 64, (1, 1): 64}


def tile_list_hscat_m_gelu_kernel(tc, x, w1, w2_words, w2_scales, b, wgo, offs, out):
    nc = tc.nc
    with ExitStack() as ctx:
        keep = ctx.enter_context(tc.tile_pool(name="keep", bufs=1))
        psum = ctx.enter_context(tc.psum_pool(name="psum", bufs=1))
        placed = ctx.enter_context(tc.tile_pool(name="placed", bufs=1))
        landed = ctx.enter_context(tc.tile_pool(name="landed", bufs=1))

        def place(shape, dtype, name, where):
            if isinstance(where, int):
                return placed.tile(shape, dtype, name=name, align_bytes=64, offset=where)
            return keep.tile(shape, dtype, name=name, tag=where, align_bytes=64)

        offsets = keep.tile([P, S // 16], U16, name="offsets")
        windows = [landed.tile([P, T], F32, name="window%d" % c, align_bytes=256) for c in range(OUT_TILES)]

        b_rows = keep.tile([P, P], F32, name="b_rows", align_bytes=64)
        nc.scalar.dma_start(
            out=b_rows[31:P:32, :].rearrange("q (c i) -> q c i", i=32),
            in_=b.rearrange("(c q i) -> q c i", c=OUT_TILES, i=32),
        )
        for q in range(4):
            nc.vector.memset(b_rows[32 * q : 32 * q + 31, :], 0.0)
        zero_in = keep.tile([P, 1], F32, name="zero_in")
        nc.vector.memset(zero_in[:], 0.0)
        w2_plane = keep.tile([P, M], U8, name="w2_plane", align_bytes=64)
        nc.vector.memset(w2_plane[:].bitcast(I32), 0)

        w1_raw = {}
        x_raw = {}

        def load_w1(a, c0, cols):
            raw = landed.tile([P, PACK, cols], F32, name="w1_raw%d_%d" % (a, c0), align_bytes=256)
            nc.sync.dma_start(
                out=raw[:],
                in_=w1[a * K_PASS : (a + 1) * K_PASS, c0 : c0 + cols].rearrange("(p j) c -> p j c", j=PACK),
            )
            w1_raw[(a, c0)] = raw

        def load_x(h, a):
            raw = landed.tile([P, PACK, HALF], F32, name="x_raw%d%d" % (h, a), align_bytes=256)
            nc.sync.dma_start(
                out=raw[:],
                in_=x[a * K_PASS : (a + 1) * K_PASS, h * HALF : (h + 1) * HALF].rearrange("(p j) c -> p j c", j=PACK),
            )
            x_raw[(h, a)] = raw

        load_x(0, 0)
        load_w1(0, 0, 256)
        load_w1(0, 256, 256)
        load_w1(1, 0, 256)
        load_w1(1, 256, 128)
        load_x(0, 1)
        load_w1(1, 384, 128)
        load_x(1, 0)
        for q in range(4):
            nc.sync.dma_start(
                out=w2_plane[32 * q : 32 * q + 4, :].bitcast(I32),
                in_=w2_scales[0, 4 * q : 4 * q + 4, :].bitcast(I32),
            )
        load_x(1, 1)
        w2_codes = [landed.tile([P, M], U8, name="w2_codes%d" % h, align_bytes=256) for h in range(2)]
        weights = [placed.tile([P, HALF], F32, name="weights%d" % h, align_bytes=256, offset=h * ROW) for h in range(2)]

        def load_second(h):
            nc.sync.dma_start(out=w2_codes[h][:].bitcast(I32), in_=w2_words[0, :, h * M : (h + 1) * M].bitcast(I32))
            nc.sync.dma_start(out=weights[h][:], in_=wgo[:, h * HALF : (h + 1) * HALF])

        load_second(0)
        nc.sync.dma_start(offsets[:], offs)
        load_second(1)

        bias = keep.tile([P, P], F32, name="bias", align_bytes=64)
        zero = keep.tile([P, 1], F32, name="zero")
        nc.scalar.activation(out=zero[:], in_=zero_in[:], func=ACT.Gelu_apprx_tanh)
        nc.vector.transpose(bias[:], b_rows[:])

        for window in windows:
            nc.vector.memset(window[:], 0.0)

        w1_codes = {}
        w1_plane = {}
        all_codes = keep.tile([P, PASSES * R], U32, name="w1_codes", align_bytes=64)
        all_plane = keep.tile([P, PASSES * R], U8, name="w1_plane", align_bytes=64)
        for a in range(PASSES):
            w1_codes[a] = all_codes[:, a * R : (a + 1) * R]
            w1_plane[a] = all_plane[:, a * R : (a + 1) * R]

        def group(a, t):
            return (t + a) % PACK * P

        def warm_up(first, cols):
            nc.tensor.matmul_mx(
                out=unread[:, 0:cols],
                lhsT=xa0[0][:, 0:WARM_ROWS].bitcast(FP8X4),
                lhsT_scale=xa0[1][:, 0:WARM_ROWS],
                rhs=all_codes[:, first : first + cols].bitcast(FP8X4),
                rhs_scale=all_plane[:, 0:cols],
                start=True,
                stop=True,
            )

        def quantise_w1(a, pieces):
            first = pieces[0][0]
            ms = sum(cols for c0, cols in pieces) // PACK
            part_v = keep.tile([P, 2, ms, PACK], BF16, name="w1_v%d_%d" % (a, first), align_bytes=64)
            part_s = keep.tile([P, 2, ms, PACK], BF16, name="w1_s%d_%d" % (a, first), align_bytes=64)
            for c0, cols in pieces:
                src = w1_raw[(a, c0)][:].rearrange("p j (m t) -> p m j t", t=PACK)
                here = slice((c0 - first) // PACK, (c0 - first + cols) // PACK)
                nc.vector.tensor_copy(out=part_v[:, :, here].rearrange("p t m j -> p m j t"), in_=src[:, :, :, 0:2])
                nc.scalar.copy(out=part_s[:, :, here].rearrange("p t m j -> p m j t"), in_=src[:, :, :, 2:PACK])
            m0 = first // PACK
            for t in range(PACK):
                grouped = part_v[:, t] if t < 2 else part_s[:, t - 2]
                nc.vector.quantize_mx(
                    out=w1_codes[a][:, group(a, t) + m0 : group(a, t) + m0 + ms].bitcast(FP8X4),
                    scales=w1_plane[a][:, group(a, t) + m0 : group(a, t) + m0 + ms],
                    in_=grouped.rearrange("p m j -> p (m j)"),
                )

        def round_x(h, a, tag):
            grouped = keep.tile([P, HALF, PACK], BF16, name="x_grouped%d%d" % (h, a), tag=tag, align_bytes=64)
            dst = grouped[:].rearrange("p (c i) j -> p c j i", i=4)
            src = x_raw[(h, a)][:].rearrange("p j (c i) -> p c j i", i=4)
            cut = X_ON_VECTOR[(h, a)] // 4
            if cut > 0:
                nc.vector.tensor_copy(out=dst[:, 0:cut], in_=src[:, 0:cut])
            if cut < HALF // 4:
                nc.scalar.copy(out=dst[:, cut:], in_=src[:, cut:])
            return grouped

        def quantise(name, grouped, tag):
            codes = place([P, HALF], U32, name + "_codes", tag)
            plane = keep.tile([P, HALF], U8, name=name + "_plane", align_bytes=64)
            nc.vector.quantize_mx(
                out=codes[:].bitcast(FP8X4),
                scales=plane[:],
                in_=grouped[:].rearrange("p c j -> p (c j)"),
            )
            return codes, plane

        def first_product(banks, a, operand):
            codes, plane = operand
            per_bank = PACK // len(banks)
            for t in range(PACK):
                nc.tensor.matmul_mx(
                    out=banks[t // per_bank][:, t % per_bank, :],
                    lhsT=w1_codes[a][:, group(a, t) : group(a, t) + P].bitcast(FP8X4),
                    lhsT_scale=w1_plane[a][:, group(a, t) : group(a, t) + P],
                    rhs=codes[:].bitcast(FP8X4),
                    rhs_scale=plane[:],
                    start=(a == 0 and t % per_bank == 0),
                    stop=(a == PASSES - 1 and t % per_bank == per_bank - 1),
                )

        acts = {}

        def second_product(h, tiles, operand, bank_tag, act_tag):
            codes, plane = operand
            acc = psum.tile([P, len(tiles), HALF], F32, name="y%d%d" % (h, tiles[0]), tag=bank_tag)
            act = place([P, len(tiles), HALF], F32, "act%d%d" % (h, tiles[0]), act_tag)
            for i, c in enumerate(tiles):
                nc.tensor.matmul_mx(
                    out=acc[:, i, :],
                    lhsT=w2_codes[c // 2][:, 2 * P * (c % 2) : 2 * P * (c % 2 + 1)].bitcast(FP4X4),
                    lhsT_scale=w2_plane[:, P * c : P * (c + 1)],
                    rhs=codes[:].bitcast(FP8X4),
                    rhs_scale=plane[:],
                    start=True,
                    stop=True,
                )
            for i, c in enumerate(tiles):
                nc.scalar.activation(out=act[:, i, :], in_=acc[:, i, :], func=ACT.Gelu_apprx_tanh, bias=bias[:, 32 * c + 31 : 32 * c + 32])
                acts[(h, c)] = act[:, i, :]

        def scatter(h, c):
            nc.vector.tensor_tensor(
                windows[c][:].indirect(offsets[:, h * HALF // 16 : (h + 1) * HALF // 16]),
                acts[(h, c)],
                weights[h][:],
                MULT,
            )

        ha_low = psum.tile([P, 2, HALF], F32, name="ha_low")
        ha_high = psum.tile([P, 2, HALF], F32, name="ha_high")
        hb = psum.tile([P, PACK, HALF], F32, name="hb")
        xa0 = quantise("xa0", round_x(0, 0, "xa0_rounded"), "xa0_codes")
        quantise_w1(0, [(0, 256)])
        quantise_w1(0, [(256, 256)])
        first_product([ha_low, ha_high], 0, xa0)
        unread = psum.tile([WARM_ROWS, R], F32, name="unread", tag="bank_y11")
        warm_up(0, R)
        quantise_w1(1, [(0, 256)])
        quantise_w1(1, [(256, 128)])
        warm_up(96, R)
        warm_up(R - 32, P)
        xa1 = quantise("xa1", round_x(0, 1, "xa1_rounded"), "xa1_codes")
        quantise_w1(1, [(384, 128)])
        first_product([ha_low, ha_high], 1, xa1)
        xb0 = quantise("xb0", round_x(1, 0, "xb0_rounded"), "xb0_codes")
        ha_grouped = keep.tile([P, HALF, PACK], BF16, name="ha_grouped", align_bytes=64)
        nc.vector.tensor_scalar_max(ha_grouped[:, :, 0:2], ha_low[:].rearrange("p t c -> p c t"), 0.0)
        ha_codes = keep.tile([P, HALF], U32, name="ha_codes", align_bytes=64)
        ha_plane = keep.tile([P, HALF], U8, name="ha_plane", align_bytes=64)
        for step in (slice(0, HALF // 2), slice(HALF // 2, HALF)):
            nc.scalar.activation(
                out=ha_grouped[:, step, 2:4], in_=ha_high[:, :, step].rearrange("p t c -> p c t"), func=ACT.Relu
            )
            nc.vector.quantize_mx(
                out=ha_codes[:, step].bitcast(FP8X4),
                scales=ha_plane[:, step],
                in_=ha_grouped[:, step].rearrange("p c j -> p (c j)"),
            )
        ha = (ha_codes, ha_plane)
        second_product(0, [0], ha, "bank_y00", ACT_AT)
        xb1 = quantise("xb1", round_x(1, 1, "xb1_rounded"), ACT_AT + 2 * ROW)
        second_product(0, [1], ha, "bank_y01", ACT_AT + ROW)
        first_product([hb], 0, xb0)
        first_product([hb], 1, xb1)
        hb_grouped = keep.tile([P, HALF, PACK], BF16, name="hb_grouped", align_bytes=64)
        nc.scalar.activation(out=hb_grouped[:], in_=hb[:].rearrange("p t c -> p c t"), func=ACT.Relu, bias=zero[:])
        scatter(0, 0)
        scatter(0, 1)
        hb_operand = quantise("hb", hb_grouped, ACT_AT)
        second_product(0, [2, 3], ha, "bank_y02", ACT_AT + 2 * ROW)
        second_product(1, [0], hb_operand, "bank_y10", ACT_AT + 4 * ROW)
        second_product(1, [1, 2, 3], hb_operand, "bank_y11", ACT_AT + 5 * ROW)
        for c in range(2, OUT_TILES):
            scatter(0, c)
        for c in range(OUT_TILES):
            scatter(1, c)
            nc.sync.dma_start(out=out[P * c : P * (c + 1), :], in_=windows[c][:])
